import numpy as np
import ml_dtypes


def mxq(x, axis, fmt="e4m3"):
    dtype, down = {"e4m3": (ml_dtypes.float8_e4m3fn, 7), "e5m2": (ml_dtypes.float8_e5m2, 14)}[fmt]
    v = np.moveaxis(np.asarray(x, np.float32).astype(ml_dtypes.bfloat16).astype(np.float64), axis, -1)
    blocks = v.reshape(v.shape[:-1] + (-1, 32))
    amax = np.abs(blocks).max(-1, keepdims=True)
    byte = np.maximum(np.where(amax > 0, np.frexp(amax)[1] - 1 + 127, 0) - down, 1)
    scale = np.exp2(byte - 127.0)
    codes = (blocks / scale).astype(np.float32).astype(dtype).astype(np.float64)
    return np.moveaxis((codes * scale).reshape(v.shape), -1, axis)


WIDE = False


def mx_kscale(k):
    if not WIDE:
        return np.ones(k)
    levels = np.array([10, -10, 5, -5, 0])
    if k % 512:
        return np.exp2(np.random.permutation(np.resize(levels, k // 32))).repeat(32)
    a = np.empty((k // 512, 16))
    for p in range(k // 512):
        a[p, :8] = np.random.permutation(np.resize(levels, 8))
        for g in range(8):
            far = levels[np.abs(levels - a[p, g]) >= 10]
            a[p, g + 8] = far[np.random.randint(len(far))]
    return np.exp2(a.ravel()).repeat(32)


def f64(x):
    return np.asarray(x).astype(np.float64)


def striped8(idx):
    return np.concatenate([x.reshape(-1, 16).T for x in idx]).astype(np.uint16)


def runs(offs, k):
    lists = np.stack([offs[16 * r : 16 * r + 16].T.reshape(-1) for r in range(8)]).astype(np.int64)
    return lists[np.arange(k) % 512 // 64]


def pack_weight(w):
    k, n = w.shape
    w = f64(np.asarray(w, np.float32).astype(ml_dtypes.bfloat16)).reshape(k // 32, 32, n)
    amax = np.abs(w).max(1)
    byte = np.clip(np.where(amax > 0, np.frexp(amax)[1] - 1 + 127 - 7, 1), 1, 254)
    scaled = (w * np.exp2(127.0 - byte)[:, None, :]).reshape(k, n).astype(np.float32)
    words = np.ascontiguousarray(scaled.reshape(k // 512, 128, 4, n).transpose(0, 1, 3, 2)).astype(ml_dtypes.float8_e4m3fn).view(np.uint8)
    return words, np.ascontiguousarray(byte.astype(np.uint8).reshape(k // 512, 16, n))


def unpack_weight(words, scales):
    g, p, n, _ = words.shape
    vals = np.ascontiguousarray(words).view(ml_dtypes.float8_e4m3fn).astype(np.float64) * np.repeat(np.exp2(scales.astype(np.float64) - 127.0), 8, axis=1)[..., None]
    return vals.transpose(0, 1, 3, 2).reshape(g * 512, n)

def planes(y):
    n, m = y.shape
    v = y.astype(np.float32).astype(ml_dtypes.bfloat16).astype(np.float64).reshape(n // 32, 32, m)
    top = np.abs(v).max(1)
    byte = np.clip(np.where(top > 0, np.frexp(top)[1] - 1 + 127 - 7, 1), 1, 254)
    codes = (v * np.exp2(127.0 - byte)[:, None, :]).reshape(n, m).astype(np.float32).astype(ml_dtypes.float8_e4m3fn).view(np.uint8)
    words = codes.reshape(n // 512, 128, 4, m).transpose(0, 1, 3, 2)
    return np.ascontiguousarray(words), np.ascontiguousarray(byte.astype(np.uint8).reshape(n // 512, 16, m))


K, T, S, N = 512, 2048, 512, 512


def setup_inputs():
    n = np.random.standard_normal
    s = mx_kscale(K)[:, None]
    packed_xT = pack_weight(n((K, T)) * s)
    return {
        "x_words": packed_xT[0],
        "x_scales": packed_xT[1],
        "w1": (n((K, N)) / np.sqrt(K) / s).astype(np.float32),
        "gamma": np.random.uniform(0.5, 1.5, (N, 1)).astype(np.float32),
        "res": n((N, S)).astype(np.float32),
        "offs": striped8(np.stack([np.random.permutation(T)[:S] for _ in range(8)])),
    }


def reference(x_words, x_scales, w1, gamma, res, offs):
    xq = unpack_weight(x_words, x_scales)[np.arange(K)[:, None], runs(offs, K)]
    h = (mxq(f64(w1), 0, "e4m3").T @ xq) + f64(res)
    hn = (h - h.mean(axis=1, keepdims=True)) / np.sqrt(h.var(axis=1, keepdims=True) + 1e-5)
    out_0 = f64(gamma) * hn
    return (out_0,) + planes(out_0)

@@ -1,0 +1,136 @@
+from contextlib import ExitStack
+
+import concourse.mybir as mybir
+
+K, T, S, N = 512, 2048, 512, 512
+FLOPS = 2 * K * S * N
+
+F32 = mybir.dt.float32
+BF16 = mybir.dt.bfloat16
+I32 = mybir.dt.int32
+U32 = mybir.dt.uint32
+U16 = mybir.dt.uint16
+U8 = mybir.dt.uint8
+FP8X4 = mybir.dt.float8_e4m3fn_x4
+ALU = mybir.AluOpType
+ACT = mybir.ActivationFunctionType
+
+P = 128
+PACK = 4
+EPS = 1e-5
+
+
+def tile_picked_phnorm_none_po_kernel(tc, x_words, x_scales, w1, gamma, res, offs, out_0, out_1, out_2):
+    nc = tc.nc
+    with ExitStack() as ctx:
+        keep = ctx.enter_context(tc.tile_pool(name="keep", bufs=1))
+        psum = ctx.enter_context(tc.psum_pool(name="psum", bufs=1))
+
+        offsets = keep.tile([P, S // 16], U16, name="offsets")
+        nc.sync.dma_start(offsets[:], offs)
+
+        scale_table = keep.tile([P, T], U8, name="scale_table", align_bytes=64)
+        nc.vector.memset(scale_table[:].bitcast(I32), 0)
+        nc.scalar.dma_start(out=scale_table[0:P:8, :].bitcast(I32), in_=x_scales[0].bitcast(I32))
+
+        word_table = keep.tile([P, T], I32, name="word_table", align_bytes=64)
+        nc.sync.dma_start(out=word_table[:], in_=x_words[0].rearrange("p c r -> p (c r)").bitcast(I32))
+
+        w_rows = w1.rearrange("(p j) m -> p j m", j=PACK)
+        half = N // 2
+        w_raw = []
+        for u in range(2):
+            w_half = keep.tile([P, PACK, half], F32, name="w_half%d" % u)
+            nc.sync.dma_start(out=w_half[:], in_=w_rows[:, :, u * half:(u + 1) * half])
+            w_raw.append(w_half)
+
+        res_rows = res.rearrange("(p t) j -> p t j", t=PACK)
+        res_sb = []
+        for u in range(2):
+            res_pair = keep.tile([P, 2, S], F32, name="res_pair%d" % u)
+            nc.sync.dma_start(out=res_pair[:], in_=res_rows[:, 2 * u:2 * u + 2, :])
+            res_sb.append(res_pair)
+
+        gamma_sb = keep.tile([P, PACK], F32, name="gamma_sb")
+        nc.gpsimd.dma_start(out=gamma_sb[:], in_=gamma.rearrange("(p t) o -> p (t o)", t=PACK))
+
+        x_scale = keep.tile([P, S], U8, name="x_scale", align_bytes=64)
+        nc.vector.memset(x_scale[:].bitcast(I32), 0)
+        warm = keep.tile([P, 2], F32, name="warm")
+        nc.vector.memset(warm[:, 0:1], 1.0)
+        nc.scalar.activation(out=warm[:, 1:2], in_=warm[:, 0:1], func=ACT.Abs_reciprocal_sqrt)
+
+        picked_scale = keep.tile([P, S], U8, name="picked_scale", align_bytes=64)
+        nc.vector.tensor_copy(out=picked_scale[:], in_=scale_table[:].indirect(offsets[:]))
+        for q in range(4):
+            nc.scalar.dma_start(out=x_scale[32 * q:32 * q + 4, :].bitcast(I32), in_=picked_scale[32 * q:32 * q + 32:8, :].bitcast(I32))
+
+        x_codes = keep.tile([P, S], U32, name="x_codes", align_bytes=64)
+        nc.vector.tensor_copy(out=x_codes[:], in_=word_table[:].bitcast(U32).indirect(offsets[:]))
+
+        w_grouped = keep.tile([P, PACK, P, PACK], BF16, name="w_grouped", align_bytes=64)
+
+        def regroup(copy, u, c0, c1):
+            base = u * (half // PACK)
+            copy(out=w_grouped[:, :, base + c0:base + c1, :].rearrange("p t c j -> p c j t"),
+                 in_=w_raw[u][:, :, PACK * c0:PACK * c1].rearrange("p j (c t) -> p c j t", t=PACK))
+
+        regroup(nc.scalar.copy, 0, 0, 64)
+        regroup(nc.vector.tensor_copy, 1, 0, 48)
+        regroup(nc.scalar.copy, 1, 48, 64)
+
+        w_codes = keep.tile([P, PACK, P], U32, name="w_codes", align_bytes=64)
+        w_scale = keep.tile([P, PACK, P], U8, name="w_scale", align_bytes=64)
+        banks = []
+        for t in range(PACK):
+            nc.vector.quantize_mx(out=w_codes[:, t, :].bitcast(FP8X4), scales=w_scale[:, t, :],
+                                  in_=w_grouped[:, t, :, :].rearrange("p c j -> p (c j)"))
+            bank = psum.tile([P, S], F32, name="bank%d" % t)
+            nc.tensor.matmul_mx(out=bank[:], lhsT=w_codes[:, t, :].bitcast(FP8X4), lhsT_scale=w_scale[:, t, :],
+                                rhs=x_codes[:].bitcast(FP8X4), rhs_scale=x_scale[:], start=True, stop=True)
+            banks.append(bank)
+
+        h = keep.tile([P, PACK, S], F32, name="h")
+        y = keep.tile([P, PACK, S], F32, name="y")
+        junk = keep.tile([P, S], BF16, name="junk")
+        out_rows = out_0.rearrange("(p t) j -> p t j", t=PACK)
+        stats = []
+        for t in range(PACK):
+            total = keep.tile([P, 1], F32, name="total%d" % t)
+            nc.vector.scalar_tensor_tensor(out=h[:, t, :], in0=banks[t][:], scalar=1.0, in1=res_sb[t // 2][:, t % 2, :],
+                                           op0=ALU.mult, op1=ALU.add, accum_out=total[:])
+            squares = keep.tile([P, 1], F32, name="squares%d" % t)
+            nc.scalar.activation(out=junk[:], in_=h[:, t, :], func=ACT.Square, scale=-float(S), bias=total[:], accum_out=squares[:])
+            rstd = keep.tile([P, 1], F32, name="rstd%d" % t)
+            nc.scalar.activation(out=rstd[:], in_=squares[:], func=ACT.Abs_reciprocal_sqrt, scale=1.0 / S ** 3, bias=EPS)
+            gain = keep.tile([P, 1], F32, name="gain%d" % t)
+            nc.scalar.activation(out=gain[:], in_=rstd[:], func=ACT.Copy, scale=gamma_sb[:, t:t + 1])
+            stats.append((total, gain))
+        for t in range(PACK):
+            total, gain = stats[t]
+            mean = keep.tile([P, 1], F32, name="mean%d" % t)
+            nc.vector.tensor_scalar(out=mean[:], in0=total[:], scalar1=1.0 / S, scalar2=None, op0=ALU.mult)
+            nc.vector.tensor_scalar(out=y[:, t, :], in0=h[:, t, :], scalar1=mean[:], scalar2=gain[:], op0=ALU.subtract, op1=ALU.mult)
+            nc.sync.dma_start(out=out_rows[:, t, :], in_=y[:, t, :])
+
+        y_grouped = keep.tile([P, S, PACK], BF16, name="y_grouped", align_bytes=64)
+
+        def weave(copy, c0, c1):
+            copy(out=y_grouped[:, c0:c1, :].rearrange("p (c i) t -> p c t i", i=4),
+                 in_=y[:, :, c0:c1].rearrange("p t (c i) -> p c t i", i=4))
+
+        weave(nc.scalar.copy, 0, 192)
+        weave(nc.vector.tensor_copy, 256, 512)
+        weave(nc.vector.tensor_copy, 192, 256)
+
+        y_codes = keep.tile([P, S], U32, name="y_codes", align_bytes=64)
+        y_scale = keep.tile([P, S], U8, name="y_scale", align_bytes=64)
+        words_out = out_1[0].rearrange("p c r -> p (c r)").bitcast(I32)
+        for c0 in (256, 0):
+            cols = slice(c0, c0 + 256)
+            nc.vector.quantize_mx(out=y_codes[:, cols].bitcast(FP8X4), scales=y_scale[:, cols],
+                                  in_=y_grouped[:, cols, :].rearrange("p c t -> p (c t)"))
+            nc.scalar.dma_start(out=words_out[:, cols], in_=y_codes[:, cols].bitcast(I32))
+        for q in range(4):
+            queue = nc.sync if q < 3 else nc.scalar
+            queue.dma_start(out=out_2[0, 4 * q:4 * q + 4, :].bitcast(I32), in_=y_scale[32 * q:32 * q + 4, :].bitcast(I32))

@@ -31,28 +31,19 @@ def tile_picked_phnorm_none_po_kernel(tc, x_words, x_scales, w1, gamma, res, off
 
         scale_table = keep.tile([P, T], U8, name="scale_table", align_bytes=64)
         nc.vector.memset(scale_table[:].bitcast(I32), 0)
-        nc.scalar.dma_start(out=scale_table[0:P:8, :].bitcast(I32), in_=x_scales[0].bitcast(I32))
+
+        w_rows = w1.rearrange("(p j) m -> p j m", j=PACK)
+        half = N // 2
+        w_raw = [keep.tile([P, PACK, half], F32, name="w_half%d" % u) for u in range(2)]
+        nc.sync.dma_start(out=w_raw[0][:], in_=w_rows[:, :, 0:half])
+        nc.sync.dma_start(out=scale_table[0:P:8, :].bitcast(I32), in_=x_scales[0].bitcast(I32))
+        nc.sync.dma_start(out=w_raw[1][:], in_=w_rows[:, :, half:N])
 
         word_table = keep.tile([P, T], I32, name="word_table", align_bytes=64)
         nc.sync.dma_start(out=word_table[:], in_=x_words[0].rearrange("p c r -> p (c r)").bitcast(I32))
 
-        w_rows = w1.rearrange("(p j) m -> p j m", j=PACK)
-        half = N // 2
-        w_raw = []
-        for u in range(2):
-            w_half = keep.tile([P, PACK, half], F32, name="w_half%d" % u)
-            nc.sync.dma_start(out=w_half[:], in_=w_rows[:, :, u * half:(u + 1) * half])
-            w_raw.append(w_half)
-
-        res_rows = res.rearrange("(p t) j -> p t j", t=PACK)
-        res_sb = []
-        for u in range(2):
-            res_pair = keep.tile([P, 2, S], F32, name="res_pair%d" % u)
-            nc.sync.dma_start(out=res_pair[:], in_=res_rows[:, 2 * u:2 * u + 2, :])
-            res_sb.append(res_pair)
-
         gamma_sb = keep.tile([P, PACK], F32, name="gamma_sb")
-        nc.gpsimd.dma_start(out=gamma_sb[:], in_=gamma.rearrange("(p t) o -> p (t o)", t=PACK))
+        nc.scalar.dma_start(out=gamma_sb[:], in_=gamma.rearrange("(p t) o -> p (t o)", t=PACK))
 
         x_scale = keep.tile([P, S], U8, name="x_scale", align_bytes=64)
         nc.vector.memset(x_scale[:].bitcast(I32), 0)
@@ -63,10 +54,14 @@ def tile_picked_phnorm_none_po_kernel(tc, x_words, x_scales, w1, gamma, res, off
         picked_scale = keep.tile([P, S], U8, name="picked_scale", align_bytes=64)
         nc.vector.tensor_copy(out=picked_scale[:], in_=scale_table[:].indirect(offsets[:]))
         for q in range(4):
-            nc.scalar.dma_start(out=x_scale[32 * q:32 * q + 4, :].bitcast(I32), in_=picked_scale[32 * q:32 * q + 32:8, :].bitcast(I32))
+            nc.sync.dma_start(out=x_scale[32 * q:32 * q + 4, :].bitcast(I32), in_=picked_scale[32 * q:32 * q + 32:8, :].bitcast(I32))
 
-        x_codes = keep.tile([P, S], U32, name="x_codes", align_bytes=64)
-        nc.vector.tensor_copy(out=x_codes[:], in_=word_table[:].bitcast(U32).indirect(offsets[:]))
+        res_rows = res.rearrange("(p t) j -> p t j", t=PACK)
+        res_sb = []
+        for u in range(2):
+            res_pair = keep.tile([P, 2, S], F32, name="res_pair%d" % u)
+            nc.sync.dma_start(out=res_pair[:], in_=res_rows[:, 2 * u:2 * u + 2, :])
+            res_sb.append(res_pair)
 
         w_grouped = keep.tile([P, PACK, P, PACK], BF16, name="w_grouped", align_bytes=64)
 
@@ -81,37 +76,60 @@ def tile_picked_phnorm_none_po_kernel(tc, x_words, x_scales, w1, gamma, res, off
 
         w_codes = keep.tile([P, PACK, P], U32, name="w_codes", align_bytes=64)
         w_scale = keep.tile([P, PACK, P], U8, name="w_scale", align_bytes=64)
-        banks = []
-        for t in range(PACK):
-            nc.vector.quantize_mx(out=w_codes[:, t, :].bitcast(FP8X4), scales=w_scale[:, t, :],
-                                  in_=w_grouped[:, t, :, :].rearrange("p c j -> p (c j)"))
-            bank = psum.tile([P, S], F32, name="bank%d" % t)
-            nc.tensor.matmul_mx(out=bank[:], lhsT=w_codes[:, t, :].bitcast(FP8X4), lhsT_scale=w_scale[:, t, :],
-                                rhs=x_codes[:].bitcast(FP8X4), rhs_scale=x_scale[:], start=True, stop=True)
-            banks.append(bank)
+        nc.vector.quantize_mx(out=w_codes[:].rearrange("p t c -> p (t c)").bitcast(FP8X4), scales=w_scale[:].rearrange("p t c -> p (t c)"),
+                              in_=w_grouped[:].rearrange("p t c j -> p (t c j)"))
+
+        places = S // 2
+        x_codes = []
+        for u in range(2):
+            picked = keep.tile([P, places], U32, name="x_codes%d" % u, align_bytes=64)
+            nc.vector.tensor_copy(out=picked[:], in_=word_table[:].bitcast(U32).indirect(offsets[:, 16 * u:16 * u + 16]))
+            x_codes.append(picked)
+
+        banks = [psum.tile([P, S], F32, name="bank%d" % t) for t in range(PACK)]
+        for t, u in ((0, 0), (1, 0), (0, 1), (1, 1), (2, 0), (2, 1), (3, 0), (3, 1)):
+            cols = slice(u * places, (u + 1) * places)
+            nc.tensor.matmul_mx(out=banks[t][:, cols], lhsT=w_codes[:, t, :].bitcast(FP8X4), lhsT_scale=w_scale[:, t, :],
+                                rhs=x_codes[u][:].bitcast(FP8X4), rhs_scale=x_scale[:, cols], start=True, stop=True)
 
         h = keep.tile([P, PACK, S], F32, name="h")
         y = keep.tile([P, PACK, S], F32, name="y")
-        junk = keep.tile([P, S], BF16, name="junk")
+        junk = keep.tile([P, PACK, S], BF16, name="junk")
         out_rows = out_0.rearrange("(p t) j -> p t j", t=PACK)
-        stats = []
-        for t in range(PACK):
-            total = keep.tile([P, 1], F32, name="total%d" % t)
-            nc.vector.scalar_tensor_tensor(out=h[:, t, :], in0=banks[t][:], scalar=1.0, in1=res_sb[t // 2][:, t % 2, :],
-                                           op0=ALU.mult, op1=ALU.add, accum_out=total[:])
-            squares = keep.tile([P, 1], F32, name="squares%d" % t)
-            nc.scalar.activation(out=junk[:], in_=h[:, t, :], func=ACT.Square, scale=-float(S), bias=total[:], accum_out=squares[:])
-            rstd = keep.tile([P, 1], F32, name="rstd%d" % t)
-            nc.scalar.activation(out=rstd[:], in_=squares[:], func=ACT.Abs_reciprocal_sqrt, scale=1.0 / S ** 3, bias=EPS)
-            gain = keep.tile([P, 1], F32, name="gain%d" % t)
-            nc.scalar.activation(out=gain[:], in_=rstd[:], func=ACT.Copy, scale=gamma_sb[:, t:t + 1])
-            stats.append((total, gain))
-        for t in range(PACK):
-            total, gain = stats[t]
-            mean = keep.tile([P, 1], F32, name="mean%d" % t)
-            nc.vector.tensor_scalar(out=mean[:], in0=total[:], scalar1=1.0 / S, scalar2=None, op0=ALU.mult)
-            nc.vector.tensor_scalar(out=y[:, t, :], in0=h[:, t, :], scalar1=mean[:], scalar2=gain[:], op0=ALU.subtract, op1=ALU.mult)
+        total = keep.tile([P, PACK], F32, name="total")
+        squares = keep.tile([P, PACK], F32, name="squares")
+        rstd = keep.tile([P, PACK], F32, name="rstd")
+        gain = keep.tile([P, PACK], F32, name="gain")
+        mean = keep.tile([P, PACK], F32, name="mean")
+        last = PACK - 1
+        split = 192
+
+        def root(ts, by):
+            nc.scalar.activation(out=rstd[:, ts], in_=squares[:, ts], func=ACT.Abs_reciprocal_sqrt, scale=by * by / S ** 3, bias=by * by * EPS)
+
+        def scaled(ts):
+            nc.vector.tensor_tensor(out=gain[:, ts], in0=rstd[:, ts], in1=gamma_sb[:, ts], op=ALU.mult)
+
+        def normalise(t):
+            nc.vector.tensor_scalar(out=y[:, t, :], in0=h[:, t, :], scalar1=mean[:, t:t + 1], scalar2=gain[:, t:t + 1], op0=ALU.subtract, op1=ALU.mult)
             nc.sync.dma_start(out=out_rows[:, t, :], in_=y[:, t, :])
+
+        for t in range(PACK):
+            nc.vector.scalar_tensor_tensor(out=h[:, t, :], in0=banks[t][:], scalar=1.0, in1=res_sb[t // 2][:, t % 2, :],
+                                           op0=ALU.mult, op1=ALU.add, accum_out=total[:, t:t + 1])
+            nc.scalar.activation(out=junk[:, t, :], in_=h[:, t, :], func=ACT.Square, scale=-float(S), bias=total[:, t:t + 1], accum_out=squares[:, t:t + 1])
+            if t > 0:
+                root(slice(0, 2) if t == 1 else slice(t, t + 1), float(S) if t == last else 1.0)
+        nc.vector.tensor_scalar(out=mean[:, 0:last], in0=total[:, 0:last], scalar1=1.0 / S, scalar2=None, op0=ALU.mult)
+        scaled(slice(0, 2))
+        centred = keep.tile([P, S], F32, name="centred")
+        nc.vector.tensor_scalar(out=centred[:], in0=h[:, last, :], scalar1=float(S), scalar2=total[:, last:PACK], op0=ALU.mult, op1=ALU.subtract)
+        normalise(0)
+        scaled(slice(2, 3))
+        normalise(1)
+        normalise(2)
+        nc.vector.tensor_scalar(out=y[:, last, :], in0=centred[:], scalar1=rstd[:, last:PACK], scalar2=gamma_sb[:, last:PACK], op0=ALU.mult, op1=ALU.mult)
+        nc.sync.dma_start(out=out_rows[:, last, :], in_=y[:, last, :])
 
         y_grouped = keep.tile([P, S, PACK], BF16, name="y_grouped", align_bytes=64)
 

@@ -26,9 +26,6 @@ def tile_picked_phnorm_none_po_kernel(tc, x_words, x_scales, w1, gamma, res, off
         keep = ctx.enter_context(tc.tile_pool(name="keep", bufs=1))
         psum = ctx.enter_context(tc.psum_pool(name="psum", bufs=1))
 
-        offsets = keep.tile([P, S // 16], U16, name="offsets")
-        nc.sync.dma_start(offsets[:], offs)
-
         scale_table = keep.tile([P, T], U8, name="scale_table", align_bytes=64)
         nc.vector.memset(scale_table[:].bitcast(I32), 0)
 
@@ -36,14 +33,14 @@ def tile_picked_phnorm_none_po_kernel(tc, x_words, x_scales, w1, gamma, res, off
         half = N // 2
         w_raw = [keep.tile([P, PACK, half], F32, name="w_half%d" % u) for u in range(2)]
         nc.sync.dma_start(out=w_raw[0][:], in_=w_rows[:, :, 0:half])
+        offsets = keep.tile([P, S // 16], U16, name="offsets")
+        nc.sync.dma_start(offsets[:], offs)
+
         nc.sync.dma_start(out=scale_table[0:P:8, :].bitcast(I32), in_=x_scales[0].bitcast(I32))
         nc.sync.dma_start(out=w_raw[1][:], in_=w_rows[:, :, half:N])
 
         word_table = keep.tile([P, T], I32, name="word_table", align_bytes=64)
         nc.sync.dma_start(out=word_table[:], in_=x_words[0].rearrange("p c r -> p (c r)").bitcast(I32))
-
-        gamma_sb = keep.tile([P, PACK], F32, name="gamma_sb")
-        nc.scalar.dma_start(out=gamma_sb[:], in_=gamma.rearrange("(p t) o -> p (t o)", t=PACK))
 
         x_scale = keep.tile([P, S], U8, name="x_scale", align_bytes=64)
         nc.vector.memset(x_scale[:].bitcast(I32), 0)
@@ -63,16 +60,18 @@ def tile_picked_phnorm_none_po_kernel(tc, x_words, x_scales, w1, gamma, res, off
             nc.sync.dma_start(out=res_pair[:], in_=res_rows[:, 2 * u:2 * u + 2, :])
             res_sb.append(res_pair)
 
+        gamma_sb = keep.tile([P, PACK], F32, name="gamma_sb")
+        nc.sync.dma_start(out=gamma_sb[:], in_=gamma.rearrange("(p t) o -> p (t o)", t=PACK))
+
         w_grouped = keep.tile([P, PACK, P, PACK], BF16, name="w_grouped", align_bytes=64)
 
         def regroup(copy, u, c0, c1):
             base = u * (half // PACK)
-            copy(out=w_grouped[:, :, base + c0:base + c1, :].rearrange("p t c j -> p c j t"),
-                 in_=w_raw[u][:, :, PACK * c0:PACK * c1].rearrange("p j (c t) -> p c j t", t=PACK))
+            copy(out=w_grouped[:, :, base + c0:base + c1, :],
+                 in_=w_raw[u][:, :, PACK * c0:PACK * c1].rearrange("p j (c t) -> p t c j", t=PACK))
 
         regroup(nc.scalar.copy, 0, 0, 64)
-        regroup(nc.vector.tensor_copy, 1, 0, 48)
-        regroup(nc.scalar.copy, 1, 48, 64)
+        regroup(nc.vector.tensor_copy, 1, 0, 64)
 
         w_codes = keep.tile([P, PACK, P], U32, name="w_codes", align_bytes=64)
         w_scale = keep.tile([P, PACK, P], U8, name="w_scale", align_bytes=64)
@@ -107,9 +106,6 @@ def tile_picked_phnorm_none_po_kernel(tc, x_words, x_scales, w1, gamma, res, off
         def root(ts, by):
             nc.scalar.activation(out=rstd[:, ts], in_=squares[:, ts], func=ACT.Abs_reciprocal_sqrt, scale=by * by / S ** 3, bias=by * by * EPS)
 
-        def scaled(ts):
-            nc.vector.tensor_tensor(out=gain[:, ts], in0=rstd[:, ts], in1=gamma_sb[:, ts], op=ALU.mult)
-
         def normalise(t):
             nc.vector.tensor_scalar(out=y[:, t, :], in0=h[:, t, :], scalar1=mean[:, t:t + 1], scalar2=gain[:, t:t + 1], op0=ALU.subtract, op1=ALU.mult)
             nc.sync.dma_start(out=out_rows[:, t, :], in_=y[:, t, :])
@@ -118,14 +114,13 @@ def tile_picked_phnorm_none_po_kernel(tc, x_words, x_scales, w1, gamma, res, off
             nc.vector.scalar_tensor_tensor(out=h[:, t, :], in0=banks[t][:], scalar=1.0, in1=res_sb[t // 2][:, t % 2, :],
                                            op0=ALU.mult, op1=ALU.add, accum_out=total[:, t:t + 1])
             nc.scalar.activation(out=junk[:, t, :], in_=h[:, t, :], func=ACT.Square, scale=-float(S), bias=total[:, t:t + 1], accum_out=squares[:, t:t + 1])
-            if t > 0:
-                root(slice(0, 2) if t == 1 else slice(t, t + 1), float(S) if t == last else 1.0)
+            root(slice(t, t + 1), float(S) if t == last else 1.0)
+            if t < last:
+                nc.scalar.activation(out=gain[:, t:t + 1], in_=rstd[:, t:t + 1], func=ACT.Copy, scale=gamma_sb[:, t:t + 1])
         nc.vector.tensor_scalar(out=mean[:, 0:last], in0=total[:, 0:last], scalar1=1.0 / S, scalar2=None, op0=ALU.mult)
-        scaled(slice(0, 2))
+        normalise(0)
         centred = keep.tile([P, S], F32, name="centred")
         nc.vector.tensor_scalar(out=centred[:], in0=h[:, last, :], scalar1=float(S), scalar2=total[:, last:PACK], op0=ALU.mult, op1=ALU.subtract)
-        normalise(0)
-        scaled(slice(2, 3))
         normalise(1)
         normalise(2)
         nc.vector.tensor_scalar(out=y[:, last, :], in0=centred[:], scalar1=rstd[:, last:PACK], scalar2=gamma_sb[:, last:PACK], op0=ALU.mult, op1=ALU.mult)

@@ -30,14 +30,13 @@ def tile_picked_phnorm_none_po_kernel(tc, x_words, x_scales, w1, gamma, res, off
         nc.vector.memset(scale_table[:].bitcast(I32), 0)
 
         w_rows = w1.rearrange("(p j) m -> p j m", j=PACK)
-        half = N // 2
-        w_raw = [keep.tile([P, PACK, half], F32, name="w_half%d" % u) for u in range(2)]
-        nc.sync.dma_start(out=w_raw[0][:], in_=w_rows[:, :, 0:half])
+        w_raw = [keep.tile([P, 2, N], F32, name="w_half%d" % u) for u in range(2)]
+        nc.sync.dma_start(out=w_raw[0][:], in_=w_rows[:, 0:2, :])
         offsets = keep.tile([P, S // 16], U16, name="offsets")
         nc.sync.dma_start(offsets[:], offs)
 
         nc.sync.dma_start(out=scale_table[0:P:8, :].bitcast(I32), in_=x_scales[0].bitcast(I32))
-        nc.sync.dma_start(out=w_raw[1][:], in_=w_rows[:, :, half:N])
+        nc.sync.dma_start(out=w_raw[1][:], in_=w_rows[:, 2:4, :])
 
         word_table = keep.tile([P, T], I32, name="word_table", align_bytes=64)
         nc.sync.dma_start(out=word_table[:], in_=x_words[0].rearrange("p c r -> p (c r)").bitcast(I32))
@@ -65,13 +64,11 @@ def tile_picked_phnorm_none_po_kernel(tc, x_words, x_scales, w1, gamma, res, off
 
         w_grouped = keep.tile([P, PACK, P, PACK], BF16, name="w_grouped", align_bytes=64)
 
-        def regroup(copy, u, c0, c1):
-            base = u * (half // PACK)
-            copy(out=w_grouped[:, :, base + c0:base + c1, :],
-                 in_=w_raw[u][:, :, PACK * c0:PACK * c1].rearrange("p j (c t) -> p t c j", t=PACK))
+        def regroup(copy, u):
+            copy(out=w_grouped[:, :, :, 2 * u:2 * u + 2], in_=w_raw[u][:].rearrange("p j (c t) -> p t c j", t=PACK))
 
-        regroup(nc.scalar.copy, 0, 0, 64)
-        regroup(nc.vector.tensor_copy, 1, 0, 64)
+        regroup(nc.scalar.copy, 0)
+        regroup(nc.vector.tensor_copy, 1)
 
         w_codes = keep.tile([P, PACK, P], U32, name="w_codes", align_bytes=64)
         w_scale = keep.tile([P, PACK, P], U8, name="w_scale", align_bytes=64)

@@ -38,7 +38,7 @@ def tile_picked_phnorm_none_po_kernel(tc, x_words, x_scales, w1, gamma, res, off
         nc.sync.dma_start(out=scale_table[0:P:8, :].bitcast(I32), in_=x_scales[0].bitcast(I32))
         nc.sync.dma_start(out=w_raw[1][:], in_=w_rows[:, 2:4, :])
 
-        word_table = keep.tile([P, T], I32, name="word_table", align_bytes=64)
+        word_table = keep.tile([P, T], I32, name="word_table", tag="words_then_codes", align_bytes=64)
         nc.sync.dma_start(out=word_table[:], in_=x_words[0].rearrange("p c r -> p (c r)").bitcast(I32))
 
         x_scale = keep.tile([P, S], U8, name="x_scale", align_bytes=64)
@@ -52,6 +52,9 @@ def tile_picked_phnorm_none_po_kernel(tc, x_words, x_scales, w1, gamma, res, off
         for q in range(4):
             nc.sync.dma_start(out=x_scale[32 * q:32 * q + 4, :].bitcast(I32), in_=picked_scale[32 * q:32 * q + 32:8, :].bitcast(I32))
 
+        gamma_sb = keep.tile([P, PACK], F32, name="gamma_sb")
+        nc.sync.dma_start(out=gamma_sb[:], in_=gamma.rearrange("(p t) o -> p (t o)", t=PACK))
+
         res_rows = res.rearrange("(p t) j -> p t j", t=PACK)
         res_sb = []
         for u in range(2):
@@ -59,21 +62,27 @@ def tile_picked_phnorm_none_po_kernel(tc, x_words, x_scales, w1, gamma, res, off
             nc.sync.dma_start(out=res_pair[:], in_=res_rows[:, 2 * u:2 * u + 2, :])
             res_sb.append(res_pair)
 
-        gamma_sb = keep.tile([P, PACK], F32, name="gamma_sb")
-        nc.sync.dma_start(out=gamma_sb[:], in_=gamma.rearrange("(p t) o -> p (t o)", t=PACK))
+        w_grouped = [keep.tile([P, 2, P, PACK], BF16, name="w_grouped%d" % v, align_bytes=64) for v in range(2)]
 
-        w_grouped = keep.tile([P, PACK, P, PACK], BF16, name="w_grouped", align_bytes=64)
+        def regroup(copy, u, v):
+            copy(out=w_grouped[v][:, :, :, 2 * u:2 * u + 2], in_=w_raw[u][:].rearrange("p j (c t) -> p t c j", t=PACK)[:, 2 * v:2 * v + 2])
 
-        def regroup(copy, u):
-            copy(out=w_grouped[:, :, :, 2 * u:2 * u + 2], in_=w_raw[u][:].rearrange("p j (c t) -> p t c j", t=PACK))
+        regroup(nc.scalar.copy, 0, 0)
+        regroup(nc.vector.tensor_copy, 1, 0)
+        regroup(nc.scalar.copy, 0, 1)
+        regroup(nc.scalar.copy, 1, 1)
 
-        regroup(nc.scalar.copy, 0)
-        regroup(nc.vector.tensor_copy, 1)
+        w_codes, w_scale = [], []
 
-        w_codes = keep.tile([P, PACK, P], U32, name="w_codes", align_bytes=64)
-        w_scale = keep.tile([P, PACK, P], U8, name="w_scale", align_bytes=64)
-        nc.vector.quantize_mx(out=w_codes[:].rearrange("p t c -> p (t c)").bitcast(FP8X4), scales=w_scale[:].rearrange("p t c -> p (t c)"),
-                              in_=w_grouped[:].rearrange("p t c j -> p (t c j)"))
+        def quantise_weights(v, tag):
+            codes = keep.tile([P, 2, P], U32, name="w_codes%d" % v, tag=tag, align_bytes=64)
+            scales = keep.tile([P, 2, P], U8, name="w_scale%d" % v, align_bytes=64)
+            nc.vector.quantize_mx(out=codes[:].rearrange("p t c -> p (t c)").bitcast(FP8X4), scales=scales[:].rearrange("p t c -> p (t c)"),
+                                  in_=w_grouped[v][:].rearrange("p t c j -> p (t c j)"))
+            w_codes.append(codes)
+            w_scale.append(scales)
+
+        quantise_weights(0, "early_codes")
 
         places = S // 2
         x_codes = []
@@ -81,11 +90,12 @@ def tile_picked_phnorm_none_po_kernel(tc, x_words, x_scales, w1, gamma, res, off
             picked = keep.tile([P, places], U32, name="x_codes%d" % u, align_bytes=64)
             nc.vector.tensor_copy(out=picked[:], in_=word_table[:].bitcast(U32).indirect(offsets[:, 16 * u:16 * u + 16]))
             x_codes.append(picked)
+        quantise_weights(1, "words_then_codes")
 
         banks = [psum.tile([P, S], F32, name="bank%d" % t) for t in range(PACK)]
         for t, u in ((0, 0), (1, 0), (0, 1), (1, 1), (2, 0), (2, 1), (3, 0), (3, 1)):
             cols = slice(u * places, (u + 1) * places)
-            nc.tensor.matmul_mx(out=banks[t][:, cols], lhsT=w_codes[:, t, :].bitcast(FP8X4), lhsT_scale=w_scale[:, t, :],
+            nc.tensor.matmul_mx(out=banks[t][:, cols], lhsT=w_codes[t // 2][:, t % 2, :].bitcast(FP8X4), lhsT_scale=w_scale[t // 2][:, t % 2, :],
                                 rhs=x_codes[u][:].bitcast(FP8X4), rhs_scale=x_scale[:, cols], start=True, stop=True)
 
         h = keep.tile([P, PACK, S], F32, name="h")
@@ -120,7 +130,8 @@ def tile_picked_phnorm_none_po_kernel(tc, x_words, x_scales, w1, gamma, res, off
         nc.vector.tensor_scalar(out=centred[:], in0=h[:, last, :], scalar1=float(S), scalar2=total[:, last:PACK], op0=ALU.mult, op1=ALU.subtract)
         normalise(1)
         normalise(2)
-        nc.vector.tensor_scalar(out=y[:, last, :], in0=centred[:], scalar1=rstd[:, last:PACK], scalar2=gamma_sb[:, last:PACK], op0=ALU.mult, op1=ALU.mult)
+        for c0, c1 in ((0, split), (256, S), (split, 256)):
+            nc.vector.tensor_scalar(out=y[:, last, c0:c1], in0=centred[:, c0:c1], scalar1=rstd[:, last:PACK], scalar2=gamma_sb[:, last:PACK], op0=ALU.mult, op1=ALU.mult)
         nc.sync.dma_start(out=out_rows[:, last, :], in_=y[:, last, :])
 
         y_grouped = keep.tile([P, S, PACK], BF16, name="y_grouped", align_bytes=64)

@@ -93,9 +93,14 @@ def tile_picked_phnorm_none_po_kernel(tc, x_words, x_scales, w1, gamma, res, off
         quantise_weights(1, "words_then_codes")
 
         banks = [psum.tile([P, S], F32, name="bank%d" % t) for t in range(PACK)]
+        second_bank = psum.tile([P, S], F32, name="second_bank")
+
+        def sums(t, cols):
+            return second_bank[:, cols] if t == 0 and cols.start > 0 else banks[t][:, cols]
+
         for t, u in ((0, 0), (1, 0), (0, 1), (1, 1), (2, 0), (2, 1), (3, 0), (3, 1)):
             cols = slice(u * places, (u + 1) * places)
-            nc.tensor.matmul_mx(out=banks[t][:, cols], lhsT=w_codes[t // 2][:, t % 2, :].bitcast(FP8X4), lhsT_scale=w_scale[t // 2][:, t % 2, :],
+            nc.tensor.matmul_mx(out=sums(t, cols), lhsT=w_codes[t // 2][:, t % 2, :].bitcast(FP8X4), lhsT_scale=w_scale[t // 2][:, t % 2, :],
                                 rhs=x_codes[u][:].bitcast(FP8X4), rhs_scale=x_scale[:, cols], start=True, stop=True)
 
         h = keep.tile([P, PACK, S], F32, name="h")
@@ -110,28 +115,60 @@ def tile_picked_phnorm_none_po_kernel(tc, x_words, x_scales, w1, gamma, res, off
         last = PACK - 1
         split = 192
 
-        def root(ts, by):
-            nc.scalar.activation(out=rstd[:, ts], in_=squares[:, ts], func=ACT.Abs_reciprocal_sqrt, scale=by * by / S ** 3, bias=by * by * EPS)
-
         def normalise(t):
-            nc.vector.tensor_scalar(out=y[:, t, :], in0=h[:, t, :], scalar1=mean[:, t:t + 1], scalar2=gain[:, t:t + 1], op0=ALU.subtract, op1=ALU.mult)
+            nc.vector.tensor_scalar(out=y[:, t, :], in0=h[:, t, :], scalar1=first_mean[:] if t == 0 else mean[:, t:t + 1], scalar2=gain[:, t:t + 1], op0=ALU.subtract, op1=ALU.mult)
             nc.sync.dma_start(out=out_rows[:, t, :], in_=y[:, t, :])
 
-        for t in range(PACK):
-            nc.vector.scalar_tensor_tensor(out=h[:, t, :], in0=banks[t][:], scalar=1.0, in1=res_sb[t // 2][:, t % 2, :],
-                                           op0=ALU.mult, op1=ALU.add, accum_out=total[:, t:t + 1])
+        def add(t, cols, into):
+            nc.vector.scalar_tensor_tensor(out=h[:, t, cols], in0=sums(t, cols), scalar=-1.0, in1=res_sb[t // 2][:, t % 2, cols],
+                                           op0=ALU.mult, op1=ALU.subtract, accum_out=into)
+
+        half_sum = keep.tile([P, 2], F32, name="half_sum")
+        shift = keep.tile([P, 1], F32, name="shift")
+        excess = keep.tile([P, 1], F32, name="excess")
+        first_mean = keep.tile([P, 1], F32, name="first_mean")
+        for u in range(2):
+            add(0, slice(u * places, (u + 1) * places), half_sum[:, u:u + 1])
+        nc.scalar.activation(out=junk[:, 0, :], in_=h[:, 0, :], func=ACT.Square, scale=-float(places), bias=half_sum[:, 0:1], accum_out=squares[:, 0:1])
+        nc.gpsimd.tensor_scalar(out=shift[:], in0=half_sum[:, 0:1], scalar1=half_sum[:, 1:2], scalar2=1.0 / S, op0=ALU.subtract, op1=ALU.mult)
+        nc.gpsimd.tensor_scalar(out=excess[:], in0=shift[:], scalar1=shift[:], scalar2=EPS, op0=ALU.mult, op1=ALU.subtract)
+        nc.gpsimd.tensor_scalar(out=first_mean[:], in0=half_sum[:, 0:1], scalar1=half_sum[:, 1:2], scalar2=1.0 / S, op0=ALU.add, op1=ALU.mult)
+        roots = [res_sb[(t + 1) // 2][:, (t + 1) % 2, 0:1] for t in range(last)] + [rstd[:, last:PACK]]
+        centred = keep.tile([P, 2, S], F32, name="centred")
+
+        def root(t):
+            if t == 0:
+                nc.scalar.activation(out=roots[0], in_=squares[:, 0:1], func=ACT.Abs_reciprocal_sqrt, scale=-1.0 / (places * places * S), bias=excess[:])
+            else:
+                by = float(S) if t >= 2 else 1.0
+                nc.scalar.activation(out=roots[t], in_=squares[:, t:t + 1], func=ACT.Abs_reciprocal_sqrt, scale=by * by / S ** 3, bias=by * by * EPS)
+
+        def centre(engine, t):
+            engine.tensor_scalar(out=centred[:, t - 2, :], in0=h[:, t, :], scalar1=-float(S), scalar2=total[:, t:t + 1], op0=ALU.mult, op1=ALU.add)
+
+        for t in range(1, PACK):
+            add(t, slice(0, S), total[:, t:t + 1])
             nc.scalar.activation(out=junk[:, t, :], in_=h[:, t, :], func=ACT.Square, scale=-float(S), bias=total[:, t:t + 1], accum_out=squares[:, t:t + 1])
-            root(slice(t, t + 1), float(S) if t == last else 1.0)
-            if t < last:
-                nc.scalar.activation(out=gain[:, t:t + 1], in_=rstd[:, t:t + 1], func=ACT.Copy, scale=gamma_sb[:, t:t + 1])
-        nc.vector.tensor_scalar(out=mean[:, 0:last], in0=total[:, 0:last], scalar1=1.0 / S, scalar2=None, op0=ALU.mult)
+            root(t - 1)
+        centre(nc.gpsimd, 2)
+        root(last)
+
+        def gain_of(t):
+            nc.vector.scalar_tensor_tensor(out=gain[:, t:t + 1], in0=roots[t], scalar=-1.0, in1=gamma_sb[:, t:t + 1], op0=ALU.mult, op1=ALU.mult)
+
+        def scale_centred(t, c0, c1):
+            nc.vector.tensor_scalar(out=y[:, t, c0:c1], in0=centred[:, t - 2, c0:c1], scalar1=roots[t], scalar2=gamma_sb[:, t:t + 1], op0=ALU.mult, op1=ALU.mult)
+
+        nc.vector.tensor_scalar(out=mean[:, 1:2], in0=total[:, 1:2], scalar1=1.0 / S, scalar2=None, op0=ALU.mult)
+        gain_of(0)
+        centre(nc.vector, last)
+        gain_of(1)
         normalise(0)
-        centred = keep.tile([P, S], F32, name="centred")
-        nc.vector.tensor_scalar(out=centred[:], in0=h[:, last, :], scalar1=float(S), scalar2=total[:, last:PACK], op0=ALU.mult, op1=ALU.subtract)
         normalise(1)
-        normalise(2)
+        scale_centred(2, 0, S)
+        nc.sync.dma_start(out=out_rows[:, 2, :], in_=y[:, 2, :])
         for c0, c1 in ((0, split), (256, S), (split, 256)):
-            nc.vector.tensor_scalar(out=y[:, last, c0:c1], in0=centred[:, c0:c1], scalar1=rstd[:, last:PACK], scalar2=gamma_sb[:, last:PACK], op0=ALU.mult, op1=ALU.mult)
+            scale_centred(last, c0, c1)
         nc.sync.dma_start(out=out_rows[:, last, :], in_=y[:, last, :])
 
         y_grouped = keep.tile([P, S, PACK], BF16, name="y_grouped", align_bytes=64)

@@ -52,15 +52,14 @@ def tile_picked_phnorm_none_po_kernel(tc, x_words, x_scales, w1, gamma, res, off
         for q in range(4):
             nc.sync.dma_start(out=x_scale[32 * q:32 * q + 4, :].bitcast(I32), in_=picked_scale[32 * q:32 * q + 32:8, :].bitcast(I32))
 
+        res_rows = res.rearrange("(p t) j -> p t j", t=PACK)
+        res_sb = [keep.tile([P, 2, S], F32, name="res_pair%d" % u) for u in range(2)]
+        nc.sync.dma_start(out=res_sb[0][:], in_=res_rows[:, 0:2, :])
+        for i in range(2):
+            nc.sync.dma_start(out=res_sb[1][:, i, :], in_=res_rows[:, 2 + i, :])
+
         gamma_sb = keep.tile([P, PACK], F32, name="gamma_sb")
         nc.sync.dma_start(out=gamma_sb[:], in_=gamma.rearrange("(p t) o -> p (t o)", t=PACK))
-
-        res_rows = res.rearrange("(p t) j -> p t j", t=PACK)
-        res_sb = []
-        for u in range(2):
-            res_pair = keep.tile([P, 2, S], F32, name="res_pair%d" % u)
-            nc.sync.dma_start(out=res_pair[:], in_=res_rows[:, 2 * u:2 * u + 2, :])
-            res_sb.append(res_pair)
 
         w_grouped = [keep.tile([P, 2, P, PACK], BF16, name="w_grouped%d" % v, align_bytes=64) for v in range(2)]
 

@@ -26,11 +26,11 @@ def tile_picked_phnorm_none_po_kernel(tc, x_words, x_scales, w1, gamma, res, off
         keep = ctx.enter_context(tc.tile_pool(name="keep", bufs=1))
         psum = ctx.enter_context(tc.psum_pool(name="psum", bufs=1))
 
-        scale_table = keep.tile([P, T], U8, name="scale_table", align_bytes=64)
+        scale_table = keep.tile([P, T], U8, name="scale_table", align_bytes=256)
         nc.vector.memset(scale_table[:].bitcast(I32), 0)
 
         w_rows = w1.rearrange("(p j) m -> p j m", j=PACK)
-        w_raw = [keep.tile([P, 2, N], F32, name="w_half%d" % u) for u in range(2)]
+        w_raw = [keep.tile([P, 2, N], F32, name="w_half%d" % u, align_bytes=256) for u in range(2)]
         nc.sync.dma_start(out=w_raw[0][:], in_=w_rows[:, 0:2, :])
         offsets = keep.tile([P, S // 16], U16, name="offsets")
         nc.sync.dma_start(offsets[:], offs)
@@ -38,30 +38,29 @@ def tile_picked_phnorm_none_po_kernel(tc, x_words, x_scales, w1, gamma, res, off
         nc.sync.dma_start(out=scale_table[0:P:8, :].bitcast(I32), in_=x_scales[0].bitcast(I32))
         nc.sync.dma_start(out=w_raw[1][:], in_=w_rows[:, 2:4, :])
 
-        word_table = keep.tile([P, T], I32, name="word_table", tag="words_then_codes", align_bytes=64)
+        word_table = keep.tile([P, T], I32, name="word_table", tag="words_then_codes", align_bytes=256)
         nc.sync.dma_start(out=word_table[:], in_=x_words[0].rearrange("p c r -> p (c r)").bitcast(I32))
 
-        x_scale = keep.tile([P, S], U8, name="x_scale", align_bytes=64)
+        x_scale = keep.tile([P, S], U8, name="x_scale", align_bytes=256)
         nc.vector.memset(x_scale[:].bitcast(I32), 0)
         warm = keep.tile([P, 2], F32, name="warm")
         nc.vector.memset(warm[:, 0:1], 1.0)
         nc.scalar.activation(out=warm[:, 1:2], in_=warm[:, 0:1], func=ACT.Abs_reciprocal_sqrt)
 
-        picked_scale = keep.tile([P, S], U8, name="picked_scale", align_bytes=64)
+        picked_scale = keep.tile([P, S], U8, name="picked_scale", align_bytes=256)
         nc.vector.tensor_copy(out=picked_scale[:], in_=scale_table[:].indirect(offsets[:]))
         for q in range(4):
             nc.sync.dma_start(out=x_scale[32 * q:32 * q + 4, :].bitcast(I32), in_=picked_scale[32 * q:32 * q + 32:8, :].bitcast(I32))
 
         res_rows = res.rearrange("(p t) j -> p t j", t=PACK)
-        res_sb = [keep.tile([P, 2, S], F32, name="res_pair%d" % u) for u in range(2)]
+        res_sb = [keep.tile([P, 2, S], F32, name="res_pair%d" % u, align_bytes=256) for u in range(2)]
         nc.sync.dma_start(out=res_sb[0][:], in_=res_rows[:, 0:2, :])
+        gamma_sb = keep.tile([P, PACK], F32, name="gamma_sb")
+        nc.sync.dma_start(out=gamma_sb[:], in_=gamma.rearrange("(p t) o -> p (t o)", t=PACK))
         for i in range(2):
             nc.sync.dma_start(out=res_sb[1][:, i, :], in_=res_rows[:, 2 + i, :])
 
-        gamma_sb = keep.tile([P, PACK], F32, name="gamma_sb")
-        nc.sync.dma_start(out=gamma_sb[:], in_=gamma.rearrange("(p t) o -> p (t o)", t=PACK))
-
-        w_grouped = [keep.tile([P, 2, P, PACK], BF16, name="w_grouped%d" % v, align_bytes=64) for v in range(2)]
+        w_grouped = [keep.tile([P, 2, P, PACK], BF16, name="w_grouped%d" % v, align_bytes=256) for v in range(2)]
 
         def regroup(copy, u, v):
             copy(out=w_grouped[v][:, :, :, 2 * u:2 * u + 2], in_=w_raw[u][:].rearrange("p j (c t) -> p t c j", t=PACK)[:, 2 * v:2 * v + 2])
@@ -74,8 +73,8 @@ def tile_picked_phnorm_none_po_kernel(tc, x_words, x_scales, w1, gamma, res, off
         w_codes, w_scale = [], []
 
         def quantise_weights(v, tag):
-            codes = keep.tile([P, 2, P], U32, name="w_codes%d" % v, tag=tag, align_bytes=64)
-            scales = keep.tile([P, 2, P], U8, name="w_scale%d" % v, align_bytes=64)
+            codes = keep.tile([P, 2, P], U32, name="w_codes%d" % v, tag=tag, align_bytes=256)
+            scales = keep.tile([P, 2, P], U8, name="w_scale%d" % v, align_bytes=256)
             nc.vector.quantize_mx(out=codes[:].rearrange("p t c -> p (t c)").bitcast(FP8X4), scales=scales[:].rearrange("p t c -> p (t c)"),
                                   in_=w_grouped[v][:].rearrange("p t c j -> p (t c j)"))
             w_codes.append(codes)
@@ -86,7 +85,7 @@ def tile_picked_phnorm_none_po_kernel(tc, x_words, x_scales, w1, gamma, res, off
         places = S // 2
         x_codes = []
         for u in range(2):
-            picked = keep.tile([P, places], U32, name="x_codes%d" % u, align_bytes=64)
+            picked = keep.tile([P, places], U32, name="x_codes%d" % u, align_bytes=256)
             nc.vector.tensor_copy(out=picked[:], in_=word_table[:].bitcast(U32).indirect(offsets[:, 16 * u:16 * u + 16]))
             x_codes.append(picked)
         quantise_weights(1, "words_then_codes")
@@ -102,9 +101,9 @@ def tile_picked_phnorm_none_po_kernel(tc, x_words, x_scales, w1, gamma, res, off
             nc.tensor.matmul_mx(out=sums(t, cols), lhsT=w_codes[t // 2][:, t % 2, :].bitcast(FP8X4), lhsT_scale=w_scale[t // 2][:, t % 2, :],
                                 rhs=x_codes[u][:].bitcast(FP8X4), rhs_scale=x_scale[:, cols], start=True, stop=True)
 
-        h = keep.tile([P, PACK, S], F32, name="h")
-        y = keep.tile([P, PACK, S], F32, name="y")
-        junk = keep.tile([P, PACK, S], BF16, name="junk")
+        h = keep.tile([P, PACK, S], F32, name="h", align_bytes=256)
+        y = keep.tile([P, PACK, S], F32, name="y", align_bytes=256)
+        junk = keep.tile([P, PACK, S], BF16, name="junk", align_bytes=256)
         out_rows = out_0.rearrange("(p t) j -> p t j", t=PACK)
         total = keep.tile([P, PACK], F32, name="total")
         squares = keep.tile([P, PACK], F32, name="squares")
@@ -130,47 +129,48 @@ def tile_picked_phnorm_none_po_kernel(tc, x_words, x_scales, w1, gamma, res, off
             add(0, slice(u * places, (u + 1) * places), half_sum[:, u:u + 1])
         nc.scalar.activation(out=junk[:, 0, :], in_=h[:, 0, :], func=ACT.Square, scale=-float(places), bias=half_sum[:, 0:1], accum_out=squares[:, 0:1])
         nc.gpsimd.tensor_scalar(out=shift[:], in0=half_sum[:, 0:1], scalar1=half_sum[:, 1:2], scalar2=1.0 / S, op0=ALU.subtract, op1=ALU.mult)
-        nc.gpsimd.tensor_scalar(out=excess[:], in0=shift[:], scalar1=shift[:], scalar2=EPS, op0=ALU.mult, op1=ALU.subtract)
         nc.gpsimd.tensor_scalar(out=first_mean[:], in0=half_sum[:, 0:1], scalar1=half_sum[:, 1:2], scalar2=1.0 / S, op0=ALU.add, op1=ALU.mult)
+        nc.gpsimd.tensor_scalar(out=excess[:], in0=shift[:], scalar1=shift[:], scalar2=EPS, op0=ALU.mult, op1=ALU.subtract)
         roots = [res_sb[(t + 1) // 2][:, (t + 1) % 2, 0:1] for t in range(last)] + [rstd[:, last:PACK]]
-        centred = keep.tile([P, 2, S], F32, name="centred")
+        centred = keep.tile([P, PACK, S], F32, name="centred", align_bytes=256)
 
         def root(t):
             if t == 0:
                 nc.scalar.activation(out=roots[0], in_=squares[:, 0:1], func=ACT.Abs_reciprocal_sqrt, scale=-1.0 / (places * places * S), bias=excess[:])
             else:
-                by = float(S) if t >= 2 else 1.0
+                by = float(S)
                 nc.scalar.activation(out=roots[t], in_=squares[:, t:t + 1], func=ACT.Abs_reciprocal_sqrt, scale=by * by / S ** 3, bias=by * by * EPS)
 
         def centre(engine, t):
-            engine.tensor_scalar(out=centred[:, t - 2, :], in0=h[:, t, :], scalar1=-float(S), scalar2=total[:, t:t + 1], op0=ALU.mult, op1=ALU.add)
+            engine.tensor_scalar(out=centred[:, t, :], in0=h[:, t, :], scalar1=-float(S), scalar2=total[:, t:t + 1], op0=ALU.mult, op1=ALU.add)
 
         for t in range(1, PACK):
             add(t, slice(0, S), total[:, t:t + 1])
             nc.scalar.activation(out=junk[:, t, :], in_=h[:, t, :], func=ACT.Square, scale=-float(S), bias=total[:, t:t + 1], accum_out=squares[:, t:t + 1])
             root(t - 1)
-        centre(nc.gpsimd, 2)
+            if t == 1:
+                centre(nc.gpsimd, 1)
         root(last)
 
         def gain_of(t):
             nc.vector.scalar_tensor_tensor(out=gain[:, t:t + 1], in0=roots[t], scalar=-1.0, in1=gamma_sb[:, t:t + 1], op0=ALU.mult, op1=ALU.mult)
 
         def scale_centred(t, c0, c1):
-            nc.vector.tensor_scalar(out=y[:, t, c0:c1], in0=centred[:, t - 2, c0:c1], scalar1=roots[t], scalar2=gamma_sb[:, t:t + 1], op0=ALU.mult, op1=ALU.mult)
+            nc.vector.tensor_scalar(out=y[:, t, c0:c1], in0=centred[:, t, c0:c1], scalar1=roots[t], scalar2=gamma_sb[:, t:t + 1], op0=ALU.mult, op1=ALU.mult)
 
-        nc.vector.tensor_scalar(out=mean[:, 1:2], in0=total[:, 1:2], scalar1=1.0 / S, scalar2=None, op0=ALU.mult)
         gain_of(0)
         centre(nc.vector, last)
-        gain_of(1)
         normalise(0)
-        normalise(1)
+        scale_centred(1, 0, S)
+        nc.sync.dma_start(out=out_rows[:, 1, :], in_=y[:, 1, :])
+        centre(nc.vector, 2)
         scale_centred(2, 0, S)
         nc.sync.dma_start(out=out_rows[:, 2, :], in_=y[:, 2, :])
         for c0, c1 in ((0, split), (256, S), (split, 256)):
             scale_centred(last, c0, c1)
         nc.sync.dma_start(out=out_rows[:, last, :], in_=y[:, last, :])
 
-        y_grouped = keep.tile([P, S, PACK], BF16, name="y_grouped", align_bytes=64)
+        y_grouped = keep.tile([P, S, PACK], BF16, name="y_grouped", align_bytes=256)
 
         def weave(copy, c0, c1):
             copy(out=y_grouped[:, c0:c1, :].rearrange("p (c i) t -> p c t i", i=4),
@@ -180,8 +180,8 @@ def tile_picked_phnorm_none_po_kernel(tc, x_words, x_scales, w1, gamma, res, off
         weave(nc.vector.tensor_copy, 256, 512)
         weave(nc.vector.tensor_copy, 192, 256)
 
-        y_codes = keep.tile([P, S], U32, name="y_codes", align_bytes=64)
-        y_scale = keep.tile([P, S], U8, name="y_scale", align_bytes=64)
+        y_codes = keep.tile([P, S], U32, name="y_codes", align_bytes=256)
+        y_scale = keep.tile([P, S], U8, name="y_scale", align_bytes=256)
         words_out = out_1[0].rearrange("p c r -> p (c r)").bitcast(I32)
         for c0 in (256, 0):
             cols = slice(c0, c0 + 256)

@@ -127,16 +127,16 @@ def tile_picked_phnorm_none_po_kernel(tc, x_words, x_scales, w1, gamma, res, off
         first_mean = keep.tile([P, 1], F32, name="first_mean")
         for u in range(2):
             add(0, slice(u * places, (u + 1) * places), half_sum[:, u:u + 1])
+        nc.scalar.activation(out=shift[:], in_=half_sum[:, 0:1], func=ACT.Square, scale=-1.0, bias=half_sum[:, 1:2])
         nc.scalar.activation(out=junk[:, 0, :], in_=h[:, 0, :], func=ACT.Square, scale=-float(places), bias=half_sum[:, 0:1], accum_out=squares[:, 0:1])
-        nc.gpsimd.tensor_scalar(out=shift[:], in0=half_sum[:, 0:1], scalar1=half_sum[:, 1:2], scalar2=1.0 / S, op0=ALU.subtract, op1=ALU.mult)
         nc.gpsimd.tensor_scalar(out=first_mean[:], in0=half_sum[:, 0:1], scalar1=half_sum[:, 1:2], scalar2=1.0 / S, op0=ALU.add, op1=ALU.mult)
-        nc.gpsimd.tensor_scalar(out=excess[:], in0=shift[:], scalar1=shift[:], scalar2=EPS, op0=ALU.mult, op1=ALU.subtract)
+        nc.scalar.activation(out=excess[:], in_=shift[:], func=ACT.Copy, bias=-S * S * EPS)
         roots = [res_sb[(t + 1) // 2][:, (t + 1) % 2, 0:1] for t in range(last)] + [rstd[:, last:PACK]]
         centred = keep.tile([P, PACK, S], F32, name="centred", align_bytes=256)
 
         def root(t):
             if t == 0:
-                nc.scalar.activation(out=roots[0], in_=squares[:, 0:1], func=ACT.Abs_reciprocal_sqrt, scale=-1.0 / (places * places * S), bias=excess[:])
+                nc.scalar.activation(out=roots[0], in_=squares[:, 0:1], func=ACT.Abs_reciprocal_sqrt, scale=-float(S) / (places * places), bias=excess[:])
             else:
                 by = float(S)
                 nc.scalar.activation(out=roots[t], in_=squares[:, t:t + 1], func=ACT.Abs_reciprocal_sqrt, scale=by * by / S ** 3, bias=by * by * EPS)
@@ -153,7 +153,7 @@ def tile_picked_phnorm_none_po_kernel(tc, x_words, x_scales, w1, gamma, res, off
         root(last)
 
         def gain_of(t):
-            nc.vector.scalar_tensor_tensor(out=gain[:, t:t + 1], in0=roots[t], scalar=-1.0, in1=gamma_sb[:, t:t + 1], op0=ALU.mult, op1=ALU.mult)
+            nc.vector.scalar_tensor_tensor(out=gain[:, t:t + 1], in0=roots[t], scalar=-float(S), in1=gamma_sb[:, t:t + 1], op0=ALU.mult, op1=ALU.mult)
 
         def scale_centred(t, c0, c1):
             nc.vector.tensor_scalar(out=y[:, t, c0:c1], in0=centred[:, t, c0:c1], scalar1=roots[t], scalar2=gamma_sb[:, t:t + 1], op0=ALU.mult, op1=ALU.mult)

@@ -17,7 +17,11 @@ ACT = mybir.ActivationFunctionType
 
 P = 128
 PACK = 4
+HALF = S // 2
+LAST = PACK - 1
 EPS = 1e-5
+ALIGN = 256
+SCALAR_PLACES = 192
 
 
 def tile_picked_phnorm_none_po_kernel(tc, x_words, x_scales, w1, gamma, res, offs, out_0, out_1, out_2):
@@ -26,11 +30,11 @@ def tile_picked_phnorm_none_po_kernel(tc, x_words, x_scales, w1, gamma, res, off
         keep = ctx.enter_context(tc.tile_pool(name="keep", bufs=1))
         psum = ctx.enter_context(tc.psum_pool(name="psum", bufs=1))
 
-        scale_table = keep.tile([P, T], U8, name="scale_table", align_bytes=256)
+        scale_table = keep.tile([P, T], U8, name="scale_table", align_bytes=ALIGN)
         nc.vector.memset(scale_table[:].bitcast(I32), 0)
 
         w_rows = w1.rearrange("(p j) m -> p j m", j=PACK)
-        w_raw = [keep.tile([P, 2, N], F32, name="w_half%d" % u, align_bytes=256) for u in range(2)]
+        w_raw = [keep.tile([P, 2, N], F32, name="w_raw%d" % u, align_bytes=ALIGN) for u in range(2)]
         nc.sync.dma_start(out=w_raw[0][:], in_=w_rows[:, 0:2, :])
         offsets = keep.tile([P, S // 16], U16, name="offsets")
         nc.sync.dma_start(offsets[:], offs)
@@ -38,43 +42,47 @@ def tile_picked_phnorm_none_po_kernel(tc, x_words, x_scales, w1, gamma, res, off
         nc.sync.dma_start(out=scale_table[0:P:8, :].bitcast(I32), in_=x_scales[0].bitcast(I32))
         nc.sync.dma_start(out=w_raw[1][:], in_=w_rows[:, 2:4, :])
 
-        word_table = keep.tile([P, T], I32, name="word_table", tag="words_then_codes", align_bytes=256)
+        word_table = keep.tile([P, T], I32, name="word_table", tag="words_then_codes", align_bytes=ALIGN)
         nc.sync.dma_start(out=word_table[:], in_=x_words[0].rearrange("p c r -> p (c r)").bitcast(I32))
 
-        x_scale = keep.tile([P, S], U8, name="x_scale", align_bytes=256)
+        x_scale = keep.tile([P, S], U8, name="x_scale", align_bytes=ALIGN)
         nc.vector.memset(x_scale[:].bitcast(I32), 0)
         warm = keep.tile([P, 2], F32, name="warm")
         nc.vector.memset(warm[:, 0:1], 1.0)
         nc.scalar.activation(out=warm[:, 1:2], in_=warm[:, 0:1], func=ACT.Abs_reciprocal_sqrt)
 
-        picked_scale = keep.tile([P, S], U8, name="picked_scale", align_bytes=256)
+        picked_scale = keep.tile([P, S], U8, name="picked_scale", align_bytes=ALIGN)
         nc.vector.tensor_copy(out=picked_scale[:], in_=scale_table[:].indirect(offsets[:]))
         for q in range(4):
             nc.sync.dma_start(out=x_scale[32 * q:32 * q + 4, :].bitcast(I32), in_=picked_scale[32 * q:32 * q + 32:8, :].bitcast(I32))
 
         res_rows = res.rearrange("(p t) j -> p t j", t=PACK)
-        res_sb = [keep.tile([P, 2, S], F32, name="res_pair%d" % u, align_bytes=256) for u in range(2)]
-        nc.sync.dma_start(out=res_sb[0][:], in_=res_rows[:, 0:2, :])
+        res_pair = [keep.tile([P, 2, S], F32, name="res_pair%d" % v, align_bytes=ALIGN) for v in range(2)]
+        nc.sync.dma_start(out=res_pair[0][:], in_=res_rows[:, 0:2, :])
         gamma_sb = keep.tile([P, PACK], F32, name="gamma_sb")
         nc.sync.dma_start(out=gamma_sb[:], in_=gamma.rearrange("(p t) o -> p (t o)", t=PACK))
         for i in range(2):
-            nc.sync.dma_start(out=res_sb[1][:, i, :], in_=res_rows[:, 2 + i, :])
+            nc.sync.dma_start(out=res_pair[1][:, i, :], in_=res_rows[:, 2 + i, :])
 
-        w_grouped = [keep.tile([P, 2, P, PACK], BF16, name="w_grouped%d" % v, align_bytes=256) for v in range(2)]
+        def res_tile(t):
+            return res_pair[t // 2][:, t % 2, :]
 
-        def regroup(copy, u, v):
-            copy(out=w_grouped[v][:, :, :, 2 * u:2 * u + 2], in_=w_raw[u][:].rearrange("p j (c t) -> p t c j", t=PACK)[:, 2 * v:2 * v + 2])
+        w_grouped = [keep.tile([P, 2, P, PACK], BF16, name="w_grouped%d" % v, align_bytes=ALIGN) for v in range(2)]
 
-        regroup(nc.scalar.copy, 0, 0)
-        regroup(nc.vector.tensor_copy, 1, 0)
-        regroup(nc.scalar.copy, 0, 1)
-        regroup(nc.scalar.copy, 1, 1)
+        def regroup(copy, u, v, cs):
+            copy(out=w_grouped[v][:, :, cs, 2 * u:2 * u + 2], in_=w_raw[u][:].rearrange("p j (c t) -> p t c j", t=PACK)[:, 2 * v:2 * v + 2, cs])
+
+        regroup(nc.scalar.copy, 0, 0, slice(0, P))
+        regroup(nc.vector.tensor_copy, 1, 0, slice(0, P))
+        regroup(nc.scalar.copy, 0, 1, slice(0, P))
+        regroup(nc.vector.tensor_copy, 1, 1, slice(0, P // 2))
+        regroup(nc.scalar.copy, 1, 1, slice(P // 2, P))
 
         w_codes, w_scale = [], []
 
         def quantise_weights(v, tag):
-            codes = keep.tile([P, 2, P], U32, name="w_codes%d" % v, tag=tag, align_bytes=256)
-            scales = keep.tile([P, 2, P], U8, name="w_scale%d" % v, align_bytes=256)
+            codes = keep.tile([P, 2, P], U32, name="w_codes%d" % v, tag=tag, align_bytes=ALIGN)
+            scales = keep.tile([P, 2, P], U8, name="w_scale%d" % v, align_bytes=ALIGN)
             nc.vector.quantize_mx(out=codes[:].rearrange("p t c -> p (t c)").bitcast(FP8X4), scales=scales[:].rearrange("p t c -> p (t c)"),
                                   in_=w_grouped[v][:].rearrange("p t c j -> p (t c j)"))
             w_codes.append(codes)
@@ -82,10 +90,10 @@ def tile_picked_phnorm_none_po_kernel(tc, x_words, x_scales, w1, gamma, res, off
 
         quantise_weights(0, "early_codes")
 
-        places = S // 2
+        halves = [slice(u * HALF, (u + 1) * HALF) for u in range(2)]
         x_codes = []
         for u in range(2):
-            picked = keep.tile([P, places], U32, name="x_codes%d" % u, align_bytes=256)
+            picked = keep.tile([P, HALF], U32, name="x_codes%d" % u, align_bytes=ALIGN)
             nc.vector.tensor_copy(out=picked[:], in_=word_table[:].bitcast(U32).indirect(offsets[:, 16 * u:16 * u + 16]))
             x_codes.append(picked)
         quantise_weights(1, "words_then_codes")
@@ -96,95 +104,88 @@ def tile_picked_phnorm_none_po_kernel(tc, x_words, x_scales, w1, gamma, res, off
         def sums(t, cols):
             return second_bank[:, cols] if t == 0 and cols.start > 0 else banks[t][:, cols]
 
-        for t, u in ((0, 0), (1, 0), (0, 1), (1, 1), (2, 0), (2, 1), (3, 0), (3, 1)):
-            cols = slice(u * places, (u + 1) * places)
-            nc.tensor.matmul_mx(out=sums(t, cols), lhsT=w_codes[t // 2][:, t % 2, :].bitcast(FP8X4), lhsT_scale=w_scale[t // 2][:, t % 2, :],
-                                rhs=x_codes[u][:].bitcast(FP8X4), rhs_scale=x_scale[:, cols], start=True, stop=True)
+        passes = [(t, u) for u in range(2) for t in range(2)] + [(t, u) for t in range(2, PACK) for u in range(2)]
+        for t, u in passes:
+            nc.tensor.matmul_mx(out=sums(t, halves[u]), lhsT=w_codes[t // 2][:, t % 2, :].bitcast(FP8X4), lhsT_scale=w_scale[t // 2][:, t % 2, :],
+                                rhs=x_codes[u][:].bitcast(FP8X4), rhs_scale=x_scale[:, halves[u]], start=True, stop=True)
 
-        h = keep.tile([P, PACK, S], F32, name="h", align_bytes=256)
-        y = keep.tile([P, PACK, S], F32, name="y", align_bytes=256)
-        junk = keep.tile([P, PACK, S], BF16, name="junk", align_bytes=256)
+        minus_h = keep.tile([P, PACK, S], F32, name="minus_h", align_bytes=ALIGN)
+        y = keep.tile([P, PACK, S], F32, name="y", align_bytes=ALIGN)
+        squared = keep.tile([P, PACK, S], BF16, name="squared", align_bytes=ALIGN)
         out_rows = out_0.rearrange("(p t) j -> p t j", t=PACK)
-        total = keep.tile([P, PACK], F32, name="total")
+        total = keep.tile([P, LAST], F32, name="total")
         squares = keep.tile([P, PACK], F32, name="squares")
-        rstd = keep.tile([P, PACK], F32, name="rstd")
-        gain = keep.tile([P, PACK], F32, name="gain")
-        mean = keep.tile([P, PACK], F32, name="mean")
-        last = PACK - 1
-        split = 192
+        last_root = keep.tile([P, 1], F32, name="last_root")
+        first_gain = keep.tile([P, 1], F32, name="first_gain")
 
-        def normalise(t):
-            nc.vector.tensor_scalar(out=y[:, t, :], in0=h[:, t, :], scalar1=first_mean[:] if t == 0 else mean[:, t:t + 1], scalar2=gain[:, t:t + 1], op0=ALU.subtract, op1=ALU.mult)
-            nc.sync.dma_start(out=out_rows[:, t, :], in_=y[:, t, :])
+        def add(t, cols, row_sum):
+            nc.vector.scalar_tensor_tensor(out=minus_h[:, t, cols], in0=sums(t, cols), scalar=-1.0, in1=res_tile(t)[:, cols],
+                                           op0=ALU.mult, op1=ALU.subtract, accum_out=row_sum)
 
-        def add(t, cols, into):
-            nc.vector.scalar_tensor_tensor(out=h[:, t, cols], in0=sums(t, cols), scalar=-1.0, in1=res_sb[t // 2][:, t % 2, cols],
-                                           op0=ALU.mult, op1=ALU.subtract, accum_out=into)
+        def square(t, count, centre_sum):
+            nc.scalar.activation(out=squared[:, t, :], in_=minus_h[:, t, :], func=ACT.Square, scale=-float(count), bias=centre_sum,
+                                 accum_out=squares[:, t:t + 1])
 
         half_sum = keep.tile([P, 2], F32, name="half_sum")
-        shift = keep.tile([P, 1], F32, name="shift")
-        excess = keep.tile([P, 1], F32, name="excess")
+        gap_squared = keep.tile([P, 1], F32, name="gap_squared")
+        gap_less_eps = keep.tile([P, 1], F32, name="gap_less_eps")
         first_mean = keep.tile([P, 1], F32, name="first_mean")
         for u in range(2):
-            add(0, slice(u * places, (u + 1) * places), half_sum[:, u:u + 1])
-        nc.scalar.activation(out=shift[:], in_=half_sum[:, 0:1], func=ACT.Square, scale=-1.0, bias=half_sum[:, 1:2])
-        nc.scalar.activation(out=junk[:, 0, :], in_=h[:, 0, :], func=ACT.Square, scale=-float(places), bias=half_sum[:, 0:1], accum_out=squares[:, 0:1])
+            add(0, halves[u], half_sum[:, u:u + 1])
+        nc.scalar.activation(out=gap_squared[:], in_=half_sum[:, 0:1], func=ACT.Square, scale=-1.0, bias=half_sum[:, 1:2])
+        square(0, HALF, half_sum[:, 0:1])
         nc.gpsimd.tensor_scalar(out=first_mean[:], in0=half_sum[:, 0:1], scalar1=half_sum[:, 1:2], scalar2=1.0 / S, op0=ALU.add, op1=ALU.mult)
-        nc.scalar.activation(out=excess[:], in_=shift[:], func=ACT.Copy, bias=-S * S * EPS)
-        roots = [res_sb[(t + 1) // 2][:, (t + 1) % 2, 0:1] for t in range(last)] + [rstd[:, last:PACK]]
-        centred = keep.tile([P, PACK, S], F32, name="centred", align_bytes=256)
+        nc.scalar.activation(out=gap_less_eps[:], in_=gap_squared[:], func=ACT.Copy, bias=-S * S * EPS)
+
+        roots = [res_tile(t + 1)[:, 0:1] for t in range(LAST)] + [last_root[:]]
+        centred = keep.tile([P, LAST, S], F32, name="centred", align_bytes=ALIGN)
 
         def root(t):
             if t == 0:
-                nc.scalar.activation(out=roots[0], in_=squares[:, 0:1], func=ACT.Abs_reciprocal_sqrt, scale=-float(S) / (places * places), bias=excess[:])
+                nc.scalar.activation(out=roots[0], in_=squares[:, 0:1], func=ACT.Abs_reciprocal_sqrt, scale=-float(S) / (HALF * HALF), bias=gap_less_eps[:])
             else:
-                by = float(S)
-                nc.scalar.activation(out=roots[t], in_=squares[:, t:t + 1], func=ACT.Abs_reciprocal_sqrt, scale=by * by / S ** 3, bias=by * by * EPS)
+                nc.scalar.activation(out=roots[t], in_=squares[:, t:t + 1], func=ACT.Abs_reciprocal_sqrt, scale=1.0 / S, bias=S * S * EPS)
 
         def centre(engine, t):
-            engine.tensor_scalar(out=centred[:, t, :], in0=h[:, t, :], scalar1=-float(S), scalar2=total[:, t:t + 1], op0=ALU.mult, op1=ALU.add)
+            engine.tensor_scalar(out=centred[:, t - 1, :], in0=minus_h[:, t, :], scalar1=-float(S), scalar2=total[:, t - 1:t], op0=ALU.mult, op1=ALU.add)
 
         for t in range(1, PACK):
-            add(t, slice(0, S), total[:, t:t + 1])
-            nc.scalar.activation(out=junk[:, t, :], in_=h[:, t, :], func=ACT.Square, scale=-float(S), bias=total[:, t:t + 1], accum_out=squares[:, t:t + 1])
+            add(t, slice(0, S), total[:, t - 1:t])
+            square(t, S, total[:, t - 1:t])
             root(t - 1)
             if t == 1:
-                centre(nc.gpsimd, 1)
-        root(last)
+                centre(nc.gpsimd, t)
+        root(LAST)
 
-        def gain_of(t):
-            nc.vector.scalar_tensor_tensor(out=gain[:, t:t + 1], in0=roots[t], scalar=-float(S), in1=gamma_sb[:, t:t + 1], op0=ALU.mult, op1=ALU.mult)
+        def scale_centred(t, cols):
+            nc.vector.tensor_scalar(out=y[:, t, cols], in0=centred[:, t - 1, cols], scalar1=roots[t], scalar2=gamma_sb[:, t:t + 1], op0=ALU.mult, op1=ALU.mult)
 
-        def scale_centred(t, c0, c1):
-            nc.vector.tensor_scalar(out=y[:, t, c0:c1], in0=centred[:, t, c0:c1], scalar1=roots[t], scalar2=gamma_sb[:, t:t + 1], op0=ALU.mult, op1=ALU.mult)
+        def store(t):
+            nc.sync.dma_start(out=out_rows[:, t, :], in_=y[:, t, :])
 
-        gain_of(0)
-        centre(nc.vector, last)
-        normalise(0)
-        scale_centred(1, 0, S)
-        nc.sync.dma_start(out=out_rows[:, 1, :], in_=y[:, 1, :])
+        nc.vector.scalar_tensor_tensor(out=first_gain[:], in0=roots[0], scalar=-float(S), in1=gamma_sb[:, 0:1], op0=ALU.mult, op1=ALU.mult)
+        centre(nc.vector, LAST)
+        nc.vector.tensor_scalar(out=y[:, 0, :], in0=minus_h[:, 0, :], scalar1=first_mean[:], scalar2=first_gain[:], op0=ALU.subtract, op1=ALU.mult)
+        store(0)
+        scale_centred(1, slice(0, S))
+        store(1)
         centre(nc.vector, 2)
-        scale_centred(2, 0, S)
-        nc.sync.dma_start(out=out_rows[:, 2, :], in_=y[:, 2, :])
-        for c0, c1 in ((0, split), (256, S), (split, 256)):
-            scale_centred(last, c0, c1)
-        nc.sync.dma_start(out=out_rows[:, last, :], in_=y[:, last, :])
+        scale_centred(2, slice(0, S))
+        store(2)
+        pieces = (slice(0, SCALAR_PLACES), halves[1], slice(SCALAR_PLACES, HALF))
+        for cols in pieces:
+            scale_centred(LAST, cols)
+        store(LAST)
 
-        y_grouped = keep.tile([P, S, PACK], BF16, name="y_grouped", align_bytes=256)
+        y_grouped = keep.tile([P, S, PACK], BF16, name="y_grouped", align_bytes=ALIGN)
+        for copy, cols in zip((nc.scalar.copy, nc.vector.tensor_copy, nc.vector.tensor_copy), pieces):
+            copy(out=y_grouped[:, cols, :].rearrange("p (c i) t -> p c t i", i=4),
+                 in_=y[:, :, cols].rearrange("p t (c i) -> p c t i", i=4))
 
-        def weave(copy, c0, c1):
-            copy(out=y_grouped[:, c0:c1, :].rearrange("p (c i) t -> p c t i", i=4),
-                 in_=y[:, :, c0:c1].rearrange("p t (c i) -> p c t i", i=4))
-
-        weave(nc.scalar.copy, 0, 192)
-        weave(nc.vector.tensor_copy, 256, 512)
-        weave(nc.vector.tensor_copy, 192, 256)
-
-        y_codes = keep.tile([P, S], U32, name="y_codes", align_bytes=256)
-        y_scale = keep.tile([P, S], U8, name="y_scale", align_bytes=256)
+        y_codes = keep.tile([P, S], U32, name="y_codes", align_bytes=ALIGN)
+        y_scale = keep.tile([P, S], U8, name="y_scale", align_bytes=ALIGN)
         words_out = out_1[0].rearrange("p c r -> p (c r)").bitcast(I32)
-        for c0 in (256, 0):
-            cols = slice(c0, c0 + 256)
+        for cols in reversed(halves):
             nc.vector.quantize_mx(out=y_codes[:, cols].bitcast(FP8X4), scales=y_scale[:, cols],
                                   in_=y_grouped[:, cols, :].rearrange("p c t -> p (c t)"))
             nc.scalar.dma_start(out=words_out[:, cols], in_=y_codes[:, cols].bitcast(I32))

@@ -1,6 +1,7 @@
 from contextlib import ExitStack
 
 import concourse.mybir as mybir
+from concourse.masks import make_identity
 
 K, T, S, N = 512, 2048, 512, 512
 FLOPS = 2 * K * S * N
@@ -42,11 +43,18 @@ def tile_picked_phnorm_none_po_kernel(tc, x_words, x_scales, w1, gamma, res, off
         nc.sync.dma_start(out=scale_table[0:P:8, :].bitcast(I32), in_=x_scales[0].bitcast(I32))
         nc.sync.dma_start(out=w_raw[1][:], in_=w_rows[:, 2:4, :])
 
+        gamma_row = keep.tile([P, N], F32, name="gamma_row", align_bytes=ALIGN)
+        nc.vector.memset(gamma_row[:], 0.0)
+        nc.sync.dma_start(out=gamma_row[0:1, :], in_=gamma.rearrange("m o -> o m"))
+
         word_table = keep.tile([P, T], I32, name="word_table", tag="words_then_codes", align_bytes=ALIGN)
         nc.sync.dma_start(out=word_table[:], in_=x_words[0].rearrange("p c r -> p (c r)").bitcast(I32))
 
         x_scale = keep.tile([P, S], U8, name="x_scale", align_bytes=ALIGN)
         nc.vector.memset(x_scale[:].bitcast(I32), 0)
+        identity = keep.tile([P, P], F32, name="identity", align_bytes=ALIGN)
+        nc.vector.memset(identity[:], 0.0)
+        make_identity(nc, identity[:], nomemset=True)
         warm = keep.tile([P, 2], F32, name="warm")
         nc.vector.memset(warm[:, 0:1], 1.0)
         nc.scalar.activation(out=warm[:, 1:2], in_=warm[:, 0:1], func=ACT.Abs_reciprocal_sqrt)
@@ -58,11 +66,8 @@ def tile_picked_phnorm_none_po_kernel(tc, x_words, x_scales, w1, gamma, res, off
 
         res_rows = res.rearrange("(p t) j -> p t j", t=PACK)
         res_pair = [keep.tile([P, 2, S], F32, name="res_pair%d" % v, align_bytes=ALIGN) for v in range(2)]
-        nc.sync.dma_start(out=res_pair[0][:], in_=res_rows[:, 0:2, :])
-        gamma_sb = keep.tile([P, PACK], F32, name="gamma_sb")
-        nc.sync.dma_start(out=gamma_sb[:], in_=gamma.rearrange("(p t) o -> p (t o)", t=PACK))
-        for i in range(2):
-            nc.sync.dma_start(out=res_pair[1][:, i, :], in_=res_rows[:, 2 + i, :])
+        for t in range(PACK):
+            nc.sync.dma_start(out=res_pair[t // 2][:, t % 2, :], in_=res_rows[:, t, :])
 
         def res_tile(t):
             return res_pair[t // 2][:, t % 2, :]
@@ -77,6 +82,12 @@ def tile_picked_phnorm_none_po_kernel(tc, x_words, x_scales, w1, gamma, res, off
         regroup(nc.scalar.copy, 0, 1, slice(0, P))
         regroup(nc.vector.tensor_copy, 1, 1, slice(0, P // 2))
         regroup(nc.scalar.copy, 1, 1, slice(P // 2, P))
+
+        turned = psum.tile([P, PACK, P], F32, name="turned")
+        for t in range(PACK):
+            nc.tensor.transpose(turned[:, t, :], gamma_row[:, t:N:PACK], identity[:])
+        gamma_sb = keep.tile([P, PACK], F32, name="gamma_sb")
+        nc.scalar.copy(out=gamma_sb[:], in_=turned[:, :, 0])
 
         w_codes, w_scale = [], []
 

@@ -33,6 +33,9 @@ def tile_picked_phnorm_none_po_kernel(tc, x_words, x_scales, w1, gamma, res, off
 
         scale_table = keep.tile([P, T], U8, name="scale_table", align_bytes=ALIGN)
         nc.vector.memset(scale_table[:].bitcast(I32), 0)
+        warm = keep.tile([P, 2], F32, name="warm")
+        nc.vector.memset(warm[:, 0:1], 1.0)
+        nc.scalar.activation(out=warm[:, 1:2], in_=warm[:, 0:1], func=ACT.Abs_reciprocal_sqrt)
 
         w_rows = w1.rearrange("(p j) m -> p j m", j=PACK)
         w_raw = [keep.tile([P, 2, N], F32, name="w_raw%d" % u, align_bytes=ALIGN) for u in range(2)]
@@ -43,6 +46,10 @@ def tile_picked_phnorm_none_po_kernel(tc, x_words, x_scales, w1, gamma, res, off
         nc.sync.dma_start(out=scale_table[0:P:8, :].bitcast(I32), in_=x_scales[0].bitcast(I32))
         nc.sync.dma_start(out=w_raw[1][:], in_=w_rows[:, 2:4, :])
 
+        identity = keep.tile([P, P], F32, name="identity", align_bytes=ALIGN)
+        nc.vector.memset(identity[:], 0.0)
+        make_identity(nc, identity[:], nomemset=True)
+
         gamma_row = keep.tile([P, N], F32, name="gamma_row", align_bytes=ALIGN)
         nc.vector.memset(gamma_row[:], 0.0)
         nc.sync.dma_start(out=gamma_row[0:1, :], in_=gamma.rearrange("m o -> o m"))
@@ -52,12 +59,6 @@ def tile_picked_phnorm_none_po_kernel(tc, x_words, x_scales, w1, gamma, res, off
 
         x_scale = keep.tile([P, S], U8, name="x_scale", align_bytes=ALIGN)
         nc.vector.memset(x_scale[:].bitcast(I32), 0)
-        identity = keep.tile([P, P], F32, name="identity", align_bytes=ALIGN)
-        nc.vector.memset(identity[:], 0.0)
-        make_identity(nc, identity[:], nomemset=True)
-        warm = keep.tile([P, 2], F32, name="warm")
-        nc.vector.memset(warm[:, 0:1], 1.0)
-        nc.scalar.activation(out=warm[:, 1:2], in_=warm[:, 0:1], func=ACT.Abs_reciprocal_sqrt)
 
         picked_scale = keep.tile([P, S], U8, name="picked_scale", align_bytes=ALIGN)
         nc.vector.tensor_copy(out=picked_scale[:], in_=scale_table[:].indirect(offsets[:]))
@@ -72,16 +73,17 @@ def tile_picked_phnorm_none_po_kernel(tc, x_words, x_scales, w1, gamma, res, off
         def res_tile(t):
             return res_pair[t // 2][:, t % 2, :]
 
-        w_grouped = [keep.tile([P, 2, P, PACK], BF16, name="w_grouped%d" % v, align_bytes=ALIGN) for v in range(2)]
+        w_grouped = keep.tile([P, PACK, P, PACK], BF16, name="w_grouped", align_bytes=ALIGN)
 
-        def regroup(copy, u, v, cs):
-            copy(out=w_grouped[v][:, :, cs, 2 * u:2 * u + 2], in_=w_raw[u][:].rearrange("p j (c t) -> p t c j", t=PACK)[:, 2 * v:2 * v + 2, cs])
+        def regroup(copy, u, tiles):
+            copy(out=w_grouped[:, tiles, :, 2 * u:2 * u + 2], in_=w_raw[u][:].rearrange("p j (c t) -> p t c j", t=PACK)[:, tiles])
 
-        regroup(nc.scalar.copy, 0, 0, slice(0, P))
-        regroup(nc.vector.tensor_copy, 1, 0, slice(0, P))
-        regroup(nc.scalar.copy, 0, 1, slice(0, P))
-        regroup(nc.vector.tensor_copy, 1, 1, slice(0, P // 2))
-        regroup(nc.scalar.copy, 1, 1, slice(P // 2, P))
+        early, late = slice(0, LAST), slice(LAST, PACK)
+        regroup(nc.scalar.copy, 0, early)
+        regroup(nc.vector.tensor_copy, 1, slice(0, 2))
+        regroup(nc.vector.tensor_copy, 1, slice(2, LAST))
+        for u in range(2):
+            regroup(nc.scalar.copy, u, late)
 
         turned = psum.tile([P, PACK, P], F32, name="turned")
         for t in range(PACK):
@@ -91,15 +93,16 @@ def tile_picked_phnorm_none_po_kernel(tc, x_words, x_scales, w1, gamma, res, off
 
         w_codes, w_scale = [], []
 
-        def quantise_weights(v, tag):
-            codes = keep.tile([P, 2, P], U32, name="w_codes%d" % v, tag=tag, align_bytes=ALIGN)
-            scales = keep.tile([P, 2, P], U8, name="w_scale%d" % v, align_bytes=ALIGN)
+        def quantise_weights(tiles, tag):
+            count = tiles.stop - tiles.start
+            codes = keep.tile([P, count, P], U32, name="w_codes%d" % tiles.start, tag=tag, align_bytes=ALIGN)
+            scales = keep.tile([P, count, P], U8, name="w_scale%d" % tiles.start, align_bytes=ALIGN)
             nc.vector.quantize_mx(out=codes[:].rearrange("p t c -> p (t c)").bitcast(FP8X4), scales=scales[:].rearrange("p t c -> p (t c)"),
-                                  in_=w_grouped[v][:].rearrange("p t c j -> p (t c j)"))
-            w_codes.append(codes)
-            w_scale.append(scales)
+                                  in_=w_grouped[:, tiles].rearrange("p t c j -> p (t c j)"))
+            w_codes.extend(codes[:, i, :] for i in range(count))
+            w_scale.extend(scales[:, i, :] for i in range(count))
 
-        quantise_weights(0, "early_codes")
+        quantise_weights(early, "early_codes")
 
         halves = [slice(u * HALF, (u + 1) * HALF) for u in range(2)]
         x_codes = []
@@ -107,7 +110,7 @@ def tile_picked_phnorm_none_po_kernel(tc, x_words, x_scales, w1, gamma, res, off
             picked = keep.tile([P, HALF], U32, name="x_codes%d" % u, align_bytes=ALIGN)
             nc.vector.tensor_copy(out=picked[:], in_=word_table[:].bitcast(U32).indirect(offsets[:, 16 * u:16 * u + 16]))
             x_codes.append(picked)
-        quantise_weights(1, "words_then_codes")
+        quantise_weights(late, "words_then_codes")
 
         banks = [psum.tile([P, S], F32, name="bank%d" % t) for t in range(PACK)]
         second_bank = psum.tile([P, S], F32, name="second_bank")
@@ -117,7 +120,7 @@ def tile_picked_phnorm_none_po_kernel(tc, x_words, x_scales, w1, gamma, res, off
 
         passes = [(t, u) for u in range(2) for t in range(2)] + [(t, u) for t in range(2, PACK) for u in range(2)]
         for t, u in passes:
-            nc.tensor.matmul_mx(out=sums(t, halves[u]), lhsT=w_codes[t // 2][:, t % 2, :].bitcast(FP8X4), lhsT_scale=w_scale[t // 2][:, t % 2, :],
+            nc.tensor.matmul_mx(out=sums(t, halves[u]), lhsT=w_codes[t].bitcast(FP8X4), lhsT_scale=w_scale[t],
                                 rhs=x_codes[u][:].bitcast(FP8X4), rhs_scale=x_scale[:, halves[u]], start=True, stop=True)
 
         minus_h = keep.tile([P, PACK, S], F32, name="minus_h", align_bytes=ALIGN)

@@ -21,8 +21,10 @@ PACK = 4
 HALF = S // 2
 LAST = PACK - 1
 EPS = 1e-5
+SPARE = 8
 ALIGN = 256
 SCALAR_PLACES = 192
+VECTOR_COLUMNS = 86
 
 
 def tile_picked_phnorm_none_po_kernel(tc, x_words, x_scales, w1, gamma, res, offs, out_0, out_1, out_2):
@@ -38,13 +40,13 @@ def tile_picked_phnorm_none_po_kernel(tc, x_words, x_scales, w1, gamma, res, off
         nc.scalar.activation(out=warm[:, 1:2], in_=warm[:, 0:1], func=ACT.Abs_reciprocal_sqrt)
 
         w_rows = w1.rearrange("(p j) m -> p j m", j=PACK)
-        w_raw = [keep.tile([P, 2, N], F32, name="w_raw%d" % u, align_bytes=ALIGN) for u in range(2)]
-        nc.sync.dma_start(out=w_raw[0][:], in_=w_rows[:, 0:2, :])
+        w_raw = keep.tile([P, PACK, N], F32, name="w_raw", align_bytes=ALIGN)
+        nc.sync.dma_start(out=w_raw[:, 0:2, :], in_=w_rows[:, 0:2, :])
         offsets = keep.tile([P, S // 16], U16, name="offsets")
         nc.sync.dma_start(offsets[:], offs)
 
         nc.sync.dma_start(out=scale_table[0:P:8, :].bitcast(I32), in_=x_scales[0].bitcast(I32))
-        nc.sync.dma_start(out=w_raw[1][:], in_=w_rows[:, 2:4, :])
+        nc.sync.dma_start(out=w_raw[:, 2:4, :], in_=w_rows[:, 2:4, :])
 
         identity = keep.tile([P, P], F32, name="identity", align_bytes=ALIGN)
         nc.vector.memset(identity[:], 0.0)
@@ -52,9 +54,9 @@ def tile_picked_phnorm_none_po_kernel(tc, x_words, x_scales, w1, gamma, res, off
 
         gamma_row = keep.tile([P, N], F32, name="gamma_row", align_bytes=ALIGN)
         nc.vector.memset(gamma_row[:], 0.0)
-        nc.sync.dma_start(out=gamma_row[0:1, :], in_=gamma.rearrange("m o -> o m"))
+        nc.sync.dma_start(out=gamma_row[1:2, :], in_=gamma.rearrange("m o -> o m"))
 
-        word_table = keep.tile([P, T], I32, name="word_table", tag="words_then_codes", align_bytes=ALIGN)
+        word_table = keep.tile([P, T], I32, name="word_table", align_bytes=ALIGN)
         nc.sync.dma_start(out=word_table[:], in_=x_words[0].rearrange("p c r -> p (c r)").bitcast(I32))
 
         x_scale = keep.tile([P, S], U8, name="x_scale", align_bytes=ALIGN)
@@ -66,43 +68,27 @@ def tile_picked_phnorm_none_po_kernel(tc, x_words, x_scales, w1, gamma, res, off
             nc.sync.dma_start(out=x_scale[32 * q:32 * q + 4, :].bitcast(I32), in_=picked_scale[32 * q:32 * q + 32:8, :].bitcast(I32))
 
         res_rows = res.rearrange("(p t) j -> p t j", t=PACK)
-        res_pair = [keep.tile([P, 2, S], F32, name="res_pair%d" % v, align_bytes=ALIGN) for v in range(2)]
+        res_tiles = [keep.tile([P, S + SPARE], F32, name="res%d" % t, align_bytes=ALIGN) for t in range(PACK)]
         for t in range(PACK):
-            nc.sync.dma_start(out=res_pair[t // 2][:, t % 2, :], in_=res_rows[:, t, :])
-
-        def res_tile(t):
-            return res_pair[t // 2][:, t % 2, :]
+            nc.sync.dma_start(out=res_tiles[t][:, 0:S], in_=res_rows[:, t, :])
 
         w_grouped = keep.tile([P, PACK, P, PACK], BF16, name="w_grouped", align_bytes=ALIGN)
+        for copy, cs in ((nc.scalar.copy, slice(VECTOR_COLUMNS, P)), (nc.vector.tensor_copy, slice(0, VECTOR_COLUMNS))):
+            copy(out=w_grouped[:].rearrange("p t c j -> p c t j")[:, cs], in_=w_raw[:].rearrange("p j (c t) -> p c t j", t=PACK)[:, cs])
 
-        def regroup(copy, u, tiles):
-            copy(out=w_grouped[:, tiles, :, 2 * u:2 * u + 2], in_=w_raw[u][:].rearrange("p j (c t) -> p t c j", t=PACK)[:, tiles])
-
-        early, late = slice(0, LAST), slice(LAST, PACK)
-        regroup(nc.scalar.copy, 0, early)
-        regroup(nc.vector.tensor_copy, 1, slice(0, 2))
-        regroup(nc.vector.tensor_copy, 1, slice(2, LAST))
-        for u in range(2):
-            regroup(nc.scalar.copy, u, late)
-
-        turned = psum.tile([P, PACK, P], F32, name="turned")
+        half_banks = [psum.tile([P, S], F32, name="half_bank%d" % u) for u in range(2)]
+        gamma_bank = psum.tile([P, S], F32, name="gamma_bank")
+        turned = [bank[:, HALF:S].rearrange("p (i c) -> p i c", i=2) for bank in (gamma_bank, half_banks[1])]
         for t in range(PACK):
-            nc.tensor.transpose(turned[:, t, :], gamma_row[:, t:N:PACK], identity[:])
-        gamma_sb = keep.tile([P, PACK], F32, name="gamma_sb")
-        nc.scalar.copy(out=gamma_sb[:], in_=turned[:, :, 0])
+            nc.tensor.transpose(turned[t // 2][:, t % 2, :], gamma_row[:, t:N:PACK], identity[:])
+        minus_gamma = keep.tile([P, 2], F32, name="minus_gamma")
+        nc.scalar.activation(out=minus_gamma[:], in_=turned[0][:, :, 1], func=ACT.Copy, scale=-1.0)
+        gains = [minus_gamma[:, 0:1], minus_gamma[:, 1:2], turned[1][:, 0, 1:2], turned[1][:, 1, 1:2]]
 
-        w_codes, w_scale = [], []
-
-        def quantise_weights(tiles, tag):
-            count = tiles.stop - tiles.start
-            codes = keep.tile([P, count, P], U32, name="w_codes%d" % tiles.start, tag=tag, align_bytes=ALIGN)
-            scales = keep.tile([P, count, P], U8, name="w_scale%d" % tiles.start, align_bytes=ALIGN)
-            nc.vector.quantize_mx(out=codes[:].rearrange("p t c -> p (t c)").bitcast(FP8X4), scales=scales[:].rearrange("p t c -> p (t c)"),
-                                  in_=w_grouped[:, tiles].rearrange("p t c j -> p (t c j)"))
-            w_codes.extend(codes[:, i, :] for i in range(count))
-            w_scale.extend(scales[:, i, :] for i in range(count))
-
-        quantise_weights(early, "early_codes")
+        w_codes = keep.tile([P, PACK, P], U32, name="w_codes", align_bytes=ALIGN)
+        w_scale = keep.tile([P, PACK, P], U8, name="w_scale", align_bytes=ALIGN)
+        nc.vector.quantize_mx(out=w_codes[:].rearrange("p t c -> p (t c)").bitcast(FP8X4), scales=w_scale[:].rearrange("p t c -> p (t c)"),
+                              in_=w_grouped[:].rearrange("p t c j -> p (t c j)"))
 
         halves = [slice(u * HALF, (u + 1) * HALF) for u in range(2)]
         x_codes = []
@@ -110,80 +96,67 @@ def tile_picked_phnorm_none_po_kernel(tc, x_words, x_scales, w1, gamma, res, off
             picked = keep.tile([P, HALF], U32, name="x_codes%d" % u, align_bytes=ALIGN)
             nc.vector.tensor_copy(out=picked[:], in_=word_table[:].bitcast(U32).indirect(offsets[:, 16 * u:16 * u + 16]))
             x_codes.append(picked)
-        quantise_weights(late, "words_then_codes")
 
-        banks = [psum.tile([P, S], F32, name="bank%d" % t) for t in range(PACK)]
-        second_bank = psum.tile([P, S], F32, name="second_bank")
+        banks = [psum.tile([P, S], F32, name="bank%d" % t) for t in range(1, PACK)]
 
-        def sums(t, cols):
-            return second_bank[:, cols] if t == 0 and cols.start > 0 else banks[t][:, cols]
+        def sums(t, u):
+            return half_banks[u][:, 0:HALF] if t == 0 else banks[t - 1][:, halves[u]]
 
         passes = [(t, u) for u in range(2) for t in range(2)] + [(t, u) for t in range(2, PACK) for u in range(2)]
         for t, u in passes:
-            nc.tensor.matmul_mx(out=sums(t, halves[u]), lhsT=w_codes[t].bitcast(FP8X4), lhsT_scale=w_scale[t],
+            nc.tensor.matmul_mx(out=sums(t, u), lhsT=w_codes[:, t, :].bitcast(FP8X4), lhsT_scale=w_scale[:, t, :],
                                 rhs=x_codes[u][:].bitcast(FP8X4), rhs_scale=x_scale[:, halves[u]], start=True, stop=True)
 
-        minus_h = keep.tile([P, PACK, S], F32, name="minus_h", align_bytes=ALIGN)
+        h = [keep.tile([P, S + SPARE], F32, name="h%d" % t, align_bytes=ALIGN) for t in range(PACK)]
+        centred = keep.tile([P, PACK, S], F32, name="centred", align_bytes=ALIGN)
         y = keep.tile([P, PACK, S], F32, name="y", align_bytes=ALIGN)
         squared = keep.tile([P, PACK, S], BF16, name="squared", align_bytes=ALIGN)
         out_rows = out_0.rearrange("(p t) j -> p t j", t=PACK)
-        total = keep.tile([P, LAST], F32, name="total")
+        total = keep.tile([P, PACK], F32, name="total")
         squares = keep.tile([P, PACK], F32, name="squares")
         last_root = keep.tile([P, 1], F32, name="last_root")
-        first_gain = keep.tile([P, 1], F32, name="first_gain")
 
-        def add(t, cols, row_sum):
-            nc.vector.scalar_tensor_tensor(out=minus_h[:, t, cols], in0=sums(t, cols), scalar=-1.0, in1=res_tile(t)[:, cols],
-                                           op0=ALU.mult, op1=ALU.subtract, accum_out=row_sum)
+        def add(t, cols, product, row_sum):
+            nc.vector.scalar_tensor_tensor(out=h[t][:, cols], in0=product, scalar=1.0, in1=res_tiles[t][:, cols],
+                                           op0=ALU.mult, op1=ALU.add, accum_out=row_sum)
 
-        def square(t, count, centre_sum):
-            nc.scalar.activation(out=squared[:, t, :], in_=minus_h[:, t, :], func=ACT.Square, scale=-float(count), bias=centre_sum,
+        def square(t):
+            nc.scalar.activation(out=squared[:, t, :], in_=h[t][:, 0:S], func=ACT.Square, scale=-float(S), bias=total[:, t:t + 1],
                                  accum_out=squares[:, t:t + 1])
 
-        half_sum = keep.tile([P, 2], F32, name="half_sum")
-        gap_squared = keep.tile([P, 1], F32, name="gap_squared")
-        gap_less_eps = keep.tile([P, 1], F32, name="gap_less_eps")
-        first_mean = keep.tile([P, 1], F32, name="first_mean")
-        for u in range(2):
-            add(0, halves[u], half_sum[:, u:u + 1])
-        nc.scalar.activation(out=gap_squared[:], in_=half_sum[:, 0:1], func=ACT.Square, scale=-1.0, bias=half_sum[:, 1:2])
-        square(0, HALF, half_sum[:, 0:1])
-        nc.gpsimd.tensor_scalar(out=first_mean[:], in0=half_sum[:, 0:1], scalar1=half_sum[:, 1:2], scalar2=1.0 / S, op0=ALU.add, op1=ALU.mult)
-        nc.scalar.activation(out=gap_less_eps[:], in_=gap_squared[:], func=ACT.Copy, bias=-S * S * EPS)
-
-        roots = [res_tile(t + 1)[:, 0:1] for t in range(LAST)] + [last_root[:]]
-        centred = keep.tile([P, LAST, S], F32, name="centred", align_bytes=ALIGN)
+        roots = [res_tiles[t + 1][:, 0:1] for t in range(LAST)] + [last_root[:]]
 
         def root(t):
-            if t == 0:
-                nc.scalar.activation(out=roots[0], in_=squares[:, 0:1], func=ACT.Abs_reciprocal_sqrt, scale=-float(S) / (HALF * HALF), bias=gap_less_eps[:])
-            else:
-                nc.scalar.activation(out=roots[t], in_=squares[:, t:t + 1], func=ACT.Abs_reciprocal_sqrt, scale=1.0 / S, bias=S * S * EPS)
+            nc.scalar.activation(out=roots[t], in_=squares[:, t:t + 1], func=ACT.Abs_reciprocal_sqrt, scale=1.0 / S, bias=S * S * EPS)
 
         def centre(engine, t):
-            engine.tensor_scalar(out=centred[:, t - 1, :], in0=minus_h[:, t, :], scalar1=-float(S), scalar2=total[:, t - 1:t], op0=ALU.mult, op1=ALU.add)
+            if t < 2:
+                engine.tensor_scalar(out=centred[:, t, :], in0=h[t][:, 0:S], scalar1=-float(S), scalar2=total[:, t:t + 1], op0=ALU.mult, op1=ALU.add)
+            else:
+                engine.tensor_scalar(out=centred[:, t, :], in0=h[t][:, 0:S], scalar1=float(S), scalar2=total[:, t:t + 1], op0=ALU.mult, op1=ALU.subtract)
 
+        add(0, slice(0, HALF), sums(0, 0), res_tiles[0][:, S:S + 1])
+        add(0, slice(HALF, S + 1), half_banks[1][:, 0:HALF + 1], total[:, 0:1])
+        square(0)
+        centre(nc.gpsimd, 0)
         for t in range(1, PACK):
-            add(t, slice(0, S), total[:, t - 1:t])
-            square(t, S, total[:, t - 1:t])
+            add(t, slice(0, S), banks[t - 1][:], total[:, t:t + 1])
+            square(t)
             root(t - 1)
             if t == 1:
                 centre(nc.gpsimd, t)
         root(LAST)
 
         def scale_centred(t, cols):
-            nc.vector.tensor_scalar(out=y[:, t, cols], in0=centred[:, t - 1, cols], scalar1=roots[t], scalar2=gamma_sb[:, t:t + 1], op0=ALU.mult, op1=ALU.mult)
+            nc.vector.tensor_scalar(out=y[:, t, cols], in0=centred[:, t, cols], scalar1=roots[t], scalar2=gains[t], op0=ALU.mult, op1=ALU.mult)
 
         def store(t):
             nc.sync.dma_start(out=out_rows[:, t, :], in_=y[:, t, :])
 
-        nc.vector.scalar_tensor_tensor(out=first_gain[:], in0=roots[0], scalar=-float(S), in1=gamma_sb[:, 0:1], op0=ALU.mult, op1=ALU.mult)
-        centre(nc.vector, LAST)
-        nc.vector.tensor_scalar(out=y[:, 0, :], in0=minus_h[:, 0, :], scalar1=first_mean[:], scalar2=first_gain[:], op0=ALU.subtract, op1=ALU.mult)
-        store(0)
-        scale_centred(1, slice(0, S))
-        store(1)
-        centre(nc.vector, 2)
+        for t in range(2):
+            scale_centred(t, slice(0, S))
+            store(t)
+            centre(nc.vector, t + 2)
         scale_centred(2, slice(0, S))
         store(2)
         pieces = (slice(0, SCALAR_PLACES), halves[1], slice(SCALAR_PLACES, HALF))

@@ -23,7 +23,7 @@ LAST = PACK - 1
 EPS = 1e-5
 SPARE = 8
 ALIGN = 256
-SCALAR_PLACES = 192
+SCALAR_PLACES = 144
 VECTOR_COLUMNS = 86
 
 
@@ -113,7 +113,8 @@ def tile_picked_phnorm_none_po_kernel(tc, x_words, x_scales, w1, gamma, res, off
         squared = keep.tile([P, PACK, S], BF16, name="squared", align_bytes=ALIGN)
         out_rows = out_0.rearrange("(p t) j -> p t j", t=PACK)
         total = keep.tile([P, PACK], F32, name="total")
-        squares = keep.tile([P, PACK], F32, name="squares")
+        first_sums = keep.tile([P, LAST], F32, name="first_sums")
+        squares = [first_sums[:, t:t + 1] for t in range(LAST)] + [y[:, 2, S - 1:S]]
         last_root = keep.tile([P, 1], F32, name="last_root")
 
         def add(t, cols, product, row_sum):
@@ -122,12 +123,12 @@ def tile_picked_phnorm_none_po_kernel(tc, x_words, x_scales, w1, gamma, res, off
 
         def square(t):
             nc.scalar.activation(out=squared[:, t, :], in_=h[t][:, 0:S], func=ACT.Square, scale=-float(S), bias=total[:, t:t + 1],
-                                 accum_out=squares[:, t:t + 1])
+                                 accum_out=squares[t])
 
         roots = [res_tiles[t + 1][:, 0:1] for t in range(LAST)] + [last_root[:]]
 
         def root(t):
-            nc.scalar.activation(out=roots[t], in_=squares[:, t:t + 1], func=ACT.Abs_reciprocal_sqrt, scale=1.0 / S, bias=S * S * EPS)
+            nc.scalar.activation(out=roots[t], in_=squares[t], func=ACT.Abs_reciprocal_sqrt, scale=1.0 / S, bias=S * S * EPS)
 
         def centre(engine, t):
             if t < 2:
@@ -157,12 +158,12 @@ def tile_picked_phnorm_none_po_kernel(tc, x_words, x_scales, w1, gamma, res, off
             scale_centred(t, slice(0, S))
             store(t)
             centre(nc.vector, t + 2)
-        scale_centred(2, slice(0, S))
+        for cols in halves:
+            for t in (2, LAST):
+                scale_centred(t, cols)
         store(2)
-        pieces = (slice(0, SCALAR_PLACES), halves[1], slice(SCALAR_PLACES, HALF))
-        for cols in pieces:
-            scale_centred(LAST, cols)
         store(LAST)
+        pieces = (slice(0, SCALAR_PLACES), slice(SCALAR_PLACES, HALF), halves[1])
 
         y_grouped = keep.tile([P, S, PACK], BF16, name="y_grouped", align_bytes=ALIGN)
         for copy, cols in zip((nc.scalar.copy, nc.vector.tensor_copy, nc.vector.tensor_copy), pieces):
@@ -172,7 +173,7 @@ def tile_picked_phnorm_none_po_kernel(tc, x_words, x_scales, w1, gamma, res, off
         y_codes = keep.tile([P, S], U32, name="y_codes", align_bytes=ALIGN)
         y_scale = keep.tile([P, S], U8, name="y_scale", align_bytes=ALIGN)
         words_out = out_1[0].rearrange("p c r -> p (c r)").bitcast(I32)
-        for cols in reversed(halves):
+        for cols in halves:
             nc.vector.quantize_mx(out=y_codes[:, cols].bitcast(FP8X4), scales=y_scale[:, cols],
                                   in_=y_grouped[:, cols, :].rearrange("p c t -> p (c t)"))
             nc.scalar.dma_start(out=words_out[:, cols], in_=y_codes[:, cols].bitcast(I32))

@@ -130,11 +130,11 @@ def tile_picked_phnorm_none_po_kernel(tc, x_words, x_scales, w1, gamma, res, off
         def root(t):
             nc.scalar.activation(out=roots[t], in_=squares[t], func=ACT.Abs_reciprocal_sqrt, scale=1.0 / S, bias=S * S * EPS)
 
-        def centre(engine, t):
+        def centre(engine, t, cols=slice(0, S)):
             if t < 2:
-                engine.tensor_scalar(out=centred[:, t, :], in0=h[t][:, 0:S], scalar1=-float(S), scalar2=total[:, t:t + 1], op0=ALU.mult, op1=ALU.add)
+                engine.tensor_scalar(out=centred[:, t, cols], in0=h[t][:, cols], scalar1=-float(S), scalar2=total[:, t:t + 1], op0=ALU.mult, op1=ALU.add)
             else:
-                engine.tensor_scalar(out=centred[:, t, :], in0=h[t][:, 0:S], scalar1=float(S), scalar2=total[:, t:t + 1], op0=ALU.mult, op1=ALU.subtract)
+                engine.tensor_scalar(out=centred[:, t, cols], in0=h[t][:, cols], scalar1=float(S), scalar2=total[:, t:t + 1], op0=ALU.mult, op1=ALU.subtract)
 
         add(0, slice(0, HALF), sums(0, 0), res_tiles[0][:, S:S + 1])
         add(0, slice(HALF, S + 1), half_banks[1][:, 0:HALF + 1], total[:, 0:1])
@@ -154,10 +154,13 @@ def tile_picked_phnorm_none_po_kernel(tc, x_words, x_scales, w1, gamma, res, off
         def store(t):
             nc.sync.dma_start(out=out_rows[:, t, :], in_=y[:, t, :])
 
-        for t in range(2):
-            scale_centred(t, slice(0, S))
-            store(t)
-            centre(nc.vector, t + 2)
+        scale_centred(0, slice(0, S))
+        store(0)
+        centre(nc.vector, LAST)
+        centre(nc.vector, 2, halves[0])
+        scale_centred(1, slice(0, S))
+        store(1)
+        centre(nc.vector, 2, halves[1])
         for cols in halves:
             for t in (2, LAST):
                 scale_centred(t, cols)

@@ -64,8 +64,8 @@ def tile_picked_phnorm_none_po_kernel(tc, x_words, x_scales, w1, gamma, res, off
 
         picked_scale = keep.tile([P, S], U8, name="picked_scale", align_bytes=ALIGN)
         nc.vector.tensor_copy(out=picked_scale[:], in_=scale_table[:].indirect(offsets[:]))
-        for q in range(4):
-            nc.sync.dma_start(out=x_scale[32 * q:32 * q + 4, :].bitcast(I32), in_=picked_scale[32 * q:32 * q + 32:8, :].bitcast(I32))
+        for i in range(4):
+            nc.sync.dma_start(out=x_scale[i:P:32, :].bitcast(I32), in_=picked_scale[8 * i:P:32, :].bitcast(I32))
 
         res_rows = res.rearrange("(p t) j -> p t j", t=PACK)
         res_tiles = [keep.tile([P, S + SPARE], F32, name="res%d" % t, align_bytes=ALIGN) for t in range(PACK)]
@@ -180,6 +180,6 @@ def tile_picked_phnorm_none_po_kernel(tc, x_words, x_scales, w1, gamma, res, off
             nc.vector.quantize_mx(out=y_codes[:, cols].bitcast(FP8X4), scales=y_scale[:, cols],
                                   in_=y_grouped[:, cols, :].rearrange("p c t -> p (c t)"))
             nc.scalar.dma_start(out=words_out[:, cols], in_=y_codes[:, cols].bitcast(I32))
-        for q in range(4):
-            queue = nc.sync if q < 3 else nc.scalar
-            queue.dma_start(out=out_2[0, 4 * q:4 * q + 4, :].bitcast(I32), in_=y_scale[32 * q:32 * q + 4, :].bitcast(I32))
+        for i in range(4):
+            queue = nc.sync if i < 3 else nc.scalar
+            queue.dma_start(out=out_2[0, i:16:4, :].bitcast(I32), in_=y_scale[i:P:32, :].bitcast(I32))

from contextlib import ExitStack

import concourse.mybir as mybir
from concourse.masks import make_identity

K, T, S, N = 512, 2048, 512, 512
FLOPS = 2 * K * S * N

F32 = mybir.dt.float32
BF16 = mybir.dt.bfloat16
I32 = mybir.dt.int32
U32 = mybir.dt.uint32
U16 = mybir.dt.uint16
U8 = mybir.dt.uint8
FP8X4 = mybir.dt.float8_e4m3fn_x4
ALU = mybir.AluOpType
ACT = mybir.ActivationFunctionType

P = 128
PACK = 4
HALF = S // 2
LAST = PACK - 1
EPS = 1e-5
SPARE = 8
ALIGN = 256
SCALAR_PLACES = 144
VECTOR_COLUMNS = 86


def tile_picked_phnorm_none_po_kernel(tc, x_words, x_scales, w1, gamma, res, offs, out_0, out_1, out_2):
    nc = tc.nc
    with ExitStack() as ctx:
        keep = ctx.enter_context(tc.tile_pool(name="keep", bufs=1))
        psum = ctx.enter_context(tc.psum_pool(name="psum", bufs=1))

        scale_table = keep.tile([P, T], U8, name="scale_table", align_bytes=ALIGN)
        nc.vector.memset(scale_table[:].bitcast(I32), 0)
        warm = keep.tile([P, 2], F32, name="warm")
        nc.vector.memset(warm[:, 0:1], 1.0)
        nc.scalar.activation(out=warm[:, 1:2], in_=warm[:, 0:1], func=ACT.Abs_reciprocal_sqrt)

        w_rows = w1.rearrange("(p j) m -> p j m", j=PACK)
        w_raw = keep.tile([P, PACK, N], F32, name="w_raw", align_bytes=ALIGN)
        nc.sync.dma_start(out=w_raw[:, 0:2, :], in_=w_rows[:, 0:2, :])
        offsets = keep.tile([P, S // 16], U16, name="offsets")
        nc.sync.dma_start(offsets[:], offs)

        nc.sync.dma_start(out=scale_table[0:P:8, :].bitcast(I32), in_=x_scales[0].bitcast(I32))
        nc.sync.dma_start(out=w_raw[:, 2:4, :], in_=w_rows[:, 2:4, :])

        identity = keep.tile([P, P], F32, name="identity", align_bytes=ALIGN)
        nc.vector.memset(identity[:], 0.0)
        make_identity(nc, identity[:], nomemset=True)

        gamma_row = keep.tile([P, N], F32, name="gamma_row", align_bytes=ALIGN)
        nc.vector.memset(gamma_row[:], 0.0)
        nc.sync.dma_start(out=gamma_row[1:2, :], in_=gamma.rearrange("m o -> o m"))

        word_table = keep.tile([P, T], I32, name="word_table", align_bytes=ALIGN)
        nc.sync.dma_start(out=word_table[:], in_=x_words[0].rearrange("p c r -> p (c r)").bitcast(I32))

        x_scale = keep.tile([P, S], U8, name="x_scale", align_bytes=ALIGN)
        nc.vector.memset(x_scale[:].bitcast(I32), 0)

        picked_scale = keep.tile([P, S], U8, name="picked_scale", align_bytes=ALIGN)
        nc.vector.tensor_copy(out=picked_scale[:], in_=scale_table[:].indirect(offsets[:]))
        for i in range(4):
            nc.sync.dma_start(out=x_scale[i:P:32, :].bitcast(I32), in_=picked_scale[8 * i:P:32, :].bitcast(I32))

        res_rows = res.rearrange("(p t) j -> p t j", t=PACK)
        res_tiles = [keep.tile([P, S + SPARE], F32, name="res%d" % t, align_bytes=ALIGN) for t in range(PACK)]
        for t in range(PACK):
            nc.sync.dma_start(out=res_tiles[t][:, 0:S], in_=res_rows[:, t, :])

        w_grouped = keep.tile([P, PACK, P, PACK], BF16, name="w_grouped", align_bytes=ALIGN)
        for copy, cs in ((nc.scalar.copy, slice(VECTOR_COLUMNS, P)), (nc.vector.tensor_copy, slice(0, VECTOR_COLUMNS))):
            copy(out=w_grouped[:].rearrange("p t c j -> p c t j")[:, cs], in_=w_raw[:].rearrange("p j (c t) -> p c t j", t=PACK)[:, cs])

        half_banks = [psum.tile([P, S], F32, name="half_bank%d" % u) for u in range(2)]
        gamma_bank = psum.tile([P, S], F32, name="gamma_bank")
        turned = [bank[:, HALF:S].rearrange("p (i c) -> p i c", i=2) for bank in (gamma_bank, half_banks[1])]
        for t in range(PACK):
            nc.tensor.transpose(turned[t // 2][:, t % 2, :], gamma_row[:, t:N:PACK], identity[:])
        minus_gamma = keep.tile([P, 2], F32, name="minus_gamma")
        nc.scalar.activation(out=minus_gamma[:], in_=turned[0][:, :, 1], func=ACT.Copy, scale=-1.0)
        gains = [minus_gamma[:, 0:1], minus_gamma[:, 1:2], turned[1][:, 0, 1:2], turned[1][:, 1, 1:2]]

        w_codes = keep.tile([P, PACK, P], U32, name="w_codes", align_bytes=ALIGN)
        w_scale = keep.tile([P, PACK, P], U8, name="w_scale", align_bytes=ALIGN)
        nc.vector.quantize_mx(out=w_codes[:].rearrange("p t c -> p (t c)").bitcast(FP8X4), scales=w_scale[:].rearrange("p t c -> p (t c)"),
                              in_=w_grouped[:].rearrange("p t c j -> p (t c j)"))

        halves = [slice(u * HALF, (u + 1) * HALF) for u in range(2)]
        x_codes = []
        for u in range(2):
            picked = keep.tile([P, HALF], U32, name="x_codes%d" % u, align_bytes=ALIGN)
            nc.vector.tensor_copy(out=picked[:], in_=word_table[:].bitcast(U32).indirect(offsets[:, 16 * u:16 * u + 16]))
            x_codes.append(picked)

        banks = [psum.tile([P, S], F32, name="bank%d" % t) for t in range(1, PACK)]

        def sums(t, u):
            return half_banks[u][:, 0:HALF] if t == 0 else banks[t - 1][:, halves[u]]

        passes = [(t, u) for u in range(2) for t in range(2)] + [(t, u) for t in range(2, PACK) for u in range(2)]
        for t, u in passes:
            nc.tensor.matmul_mx(out=sums(t, u), lhsT=w_codes[:, t, :].bitcast(FP8X4), lhsT_scale=w_scale[:, t, :],
                                rhs=x_codes[u][:].bitcast(FP8X4), rhs_scale=x_scale[:, halves[u]], start=True, stop=True)

        h = [keep.tile([P, S + SPARE], F32, name="h%d" % t, align_bytes=ALIGN) for t in range(PACK)]
        centred = keep.tile([P, PACK, S], F32, name="centred", align_bytes=ALIGN)
        y = keep.tile([P, PACK, S], F32, name="y", align_bytes=ALIGN)
        squared = keep.tile([P, PACK, S], BF16, name="squared", align_bytes=ALIGN)
        out_rows = out_0.rearrange("(p t) j -> p t j", t=PACK)
        total = keep.tile([P, PACK], F32, name="total")
        first_sums = keep.tile([P, LAST], F32, name="first_sums")
        squares = [first_sums[:, t:t + 1] for t in range(LAST)] + [y[:, 2, S - 1:S]]
        last_root = keep.tile([P, 1], F32, name="last_root")

        def add(t, cols, product, row_sum):
            nc.vector.scalar_tensor_tensor(out=h[t][:, cols], in0=product, scalar=1.0, in1=res_tiles[t][:, cols],
                                           op0=ALU.mult, op1=ALU.add, accum_out=row_sum)

        def square(t):
            nc.scalar.activation(out=squared[:, t, :], in_=h[t][:, 0:S], func=ACT.Square, scale=-float(S), bias=total[:, t:t + 1],
                                 accum_out=squares[t])

        roots = [res_tiles[t + 1][:, 0:1] for t in range(LAST)] + [last_root[:]]

        def root(t):
            nc.scalar.activation(out=roots[t], in_=squares[t], func=ACT.Abs_reciprocal_sqrt, scale=1.0 / S, bias=S * S * EPS)

        def centre(engine, t, cols=slice(0, S)):
            if t < 2:
                engine.tensor_scalar(out=centred[:, t, cols], in0=h[t][:, cols], scalar1=-float(S), scalar2=total[:, t:t + 1], op0=ALU.mult, op1=ALU.add)
            else:
                engine.tensor_scalar(out=centred[:, t, cols], in0=h[t][:, cols], scalar1=float(S), scalar2=total[:, t:t + 1], op0=ALU.mult, op1=ALU.subtract)

        add(0, slice(0, HALF), sums(0, 0), res_tiles[0][:, S:S + 1])
        add(0, slice(HALF, S + 1), half_banks[1][:, 0:HALF + 1], total[:, 0:1])
        square(0)
        centre(nc.gpsimd, 0)
        for t in range(1, PACK):
            add(t, slice(0, S), banks[t - 1][:], total[:, t:t + 1])
            square(t)
            root(t - 1)
            if t == 1:
                centre(nc.gpsimd, t)
        root(LAST)

        def scale_centred(t, cols):
            nc.vector.tensor_scalar(out=y[:, t, cols], in0=centred[:, t, cols], scalar1=roots[t], scalar2=gains[t], op0=ALU.mult, op1=ALU.mult)

        def store(t):
            nc.sync.dma_start(out=out_rows[:, t, :], in_=y[:, t, :])

        scale_centred(0, slice(0, S))
        store(0)
        centre(nc.vector, LAST)
        centre(nc.vector, 2, halves[0])
        scale_centred(1, slice(0, S))
        store(1)
        centre(nc.vector, 2, halves[1])
        for cols in halves:
            for t in (2, LAST):
                scale_centred(t, cols)
        store(2)
        store(LAST)
        pieces = (slice(0, SCALAR_PLACES), slice(SCALAR_PLACES, HALF), halves[1])

        y_grouped = keep.tile([P, S, PACK], BF16, name="y_grouped", align_bytes=ALIGN)
        for copy, cols in zip((nc.scalar.copy, nc.vector.tensor_copy, nc.vector.tensor_copy), pieces):
            copy(out=y_grouped[:, cols, :].rearrange("p (c i) t -> p c t i", i=4),
                 in_=y[:, :, cols].rearrange("p t (c i) -> p c t i", i=4))

        y_codes = keep.tile([P, S], U32, name="y_codes", align_bytes=ALIGN)
        y_scale = keep.tile([P, S], U8, name="y_scale", align_bytes=ALIGN)
        words_out = out_1[0].rearrange("p c r -> p (c r)").bitcast(I32)
        for cols in halves:
            nc.vector.quantize_mx(out=y_codes[:, cols].bitcast(FP8X4), scales=y_scale[:, cols],
                                  in_=y_grouped[:, cols, :].rearrange("p c t -> p (c t)"))
            nc.scalar.dma_start(out=words_out[:, cols], in_=y_codes[:, cols].bitcast(I32))
        for i in range(4):
            queue = nc.sync if i < 3 else nc.scalar
            queue.dma_start(out=out_2[0, i:16:4, :].bitcast(I32), in_=y_scale[i:P:32, :].bitcast(I32))
